import numpy as np
import ml_dtypes


def mxq(x, axis, fmt="e4m3"):
    dtype, down = {"e4m3": (ml_dtypes.float8_e4m3fn, 7), "e5m2": (ml_dtypes.float8_e5m2, 14)}[fmt]
    v = np.moveaxis(np.asarray(x, np.float32).astype(ml_dtypes.bfloat16).astype(np.float64), axis, -1)
    blocks = v.reshape(v.shape[:-1] + (-1, 32))
    amax = np.abs(blocks).max(-1, keepdims=True)
    byte = np.maximum(np.where(amax > 0, np.frexp(amax)[1] - 1 + 127, 0) - down, 1)
    scale = np.exp2(byte - 127.0)
    codes = (blocks / scale).astype(np.float32).astype(dtype).astype(np.float64)
    return np.moveaxis((codes * scale).reshape(v.shape), -1, axis)


WIDE = False


def mx_kscale(k):
    if not WIDE:
        return np.ones(k)
    levels = np.array([10, -10, 5, -5, 0])
    if k % 512:
        return np.exp2(np.random.permutation(np.resize(levels, k // 32))).repeat(32)
    a = np.empty((k // 512, 16))
    for p in range(k // 512):
        a[p, :8] = np.random.permutation(np.resize(levels, 8))
        for g in range(8):
            far = levels[np.abs(levels - a[p, g]) >= 10]
            a[p, g + 8] = far[np.random.randint(len(far))]
    return np.exp2(a.ravel()).repeat(32)


def f64(x):
    return np.asarray(x).astype(np.float64)


def striped8(idx):
    return np.concatenate([x.reshape(-1, 16).T for x in idx]).astype(np.uint16)


def runs(offs, k):
    lists = np.stack([offs[16 * r : 16 * r + 16].T.reshape(-1) for r in range(8)]).astype(np.int64)
    return lists[np.arange(k) % 512 // 64]


def pack_weight(w):
    k, n = w.shape
    w = f64(np.asarray(w, np.float32).astype(ml_dtypes.bfloat16)).reshape(k // 32, 32, n)
    amax = np.abs(w).max(1)
    byte = np.clip(np.where(amax > 0, np.frexp(amax)[1] - 1 + 127 - 7, 1), 1, 254)
    scaled = (w * np.exp2(127.0 - byte)[:, None, :]).reshape(k, n).astype(np.float32)
    words = np.ascontiguousarray(scaled.reshape(k // 512, 128, 4, n).transpose(0, 1, 3, 2)).astype(ml_dtypes.float8_e4m3fn).view(np.uint8)
    return words, np.ascontiguousarray(byte.astype(np.uint8).reshape(k // 512, 16, n))


def unpack_weight(words, scales):
    g, p, n, _ = words.shape
    vals = np.ascontiguousarray(words).view(ml_dtypes.float8_e4m3fn).astype(np.float64) * np.repeat(np.exp2(scales.astype(np.float64) - 127.0), 8, axis=1)[..., None]
    return vals.transpose(0, 1, 3, 2).reshape(g * 512, n)


E2M1 = np.array([0.0, 0.5, 1.0, 1.5, 2.0, 3.0, 4.0, 6.0, -0.0, -0.5, -1.0, -1.5, -2.0, -3.0, -4.0, -6.0])


def pack_fp4(w):
    k, n = w.shape
    w = f64(np.asarray(w, np.float32).astype(ml_dtypes.bfloat16)).reshape(k // 32, 32, n)
    amax = np.abs(w).max(1)
    mant, ex = np.frexp(amax / 6.0)
    byte = np.clip(np.where(amax > 0, np.where(mant > 0.5, ex, ex - 1) + 127, 1), 1, 254)
    scaled = (w * np.exp2(127.0 - byte)[:, None, :]).reshape(k, n).astype(np.float32)
    c = np.ascontiguousarray(scaled.reshape(k // 512, 128, 4, n).transpose(0, 1, 3, 2)).astype(ml_dtypes.float4_e2m1fn).view(np.uint8) & 0xF
    words = (c[..., 0::2] | (c[..., 1::2] << 4)).reshape(k // 512, 128, 2 * n)
    return np.ascontiguousarray(words), np.ascontiguousarray(byte.astype(np.uint8).reshape(k // 512, 16, n))


def unpack_fp4(words, scales):
    g, _, n = scales.shape
    words = np.ascontiguousarray(words).reshape(g, 128, n, 2)
    nib = np.empty((g, 128, n, 4), np.uint8)
    nib[..., 0::2] = words & 0xF
    nib[..., 1::2] = words >> 4
    vals = E2M1[nib] * np.repeat(np.exp2(scales.astype(np.float64) - 127.0), 8, axis=1)[..., None]
    return vals.transpose(0, 1, 3, 2).reshape(g * 512, n)


K, T, S, H, N, V = 512, 2048, 1024, 512, 128, 512


def setup_inputs():
    n = np.random.standard_normal
    s = mx_kscale(K)[:, None]
    u = mx_kscale(H)
    packed_xT = pack_weight(n((K, T)) * s)
    packed_w2 = pack_fp4(n((H, N)) / np.sqrt(H) / u[:, None])
    return {
        "x_words": packed_xT[0],
        "x_scales": packed_xT[1],
        "w1": (n((K, H)) / np.sqrt(K) / s * u).astype(np.float32),
        "w2_words": packed_w2[0],
        "w2_scales": packed_w2[1],
        "offs": striped8(np.stack([np.random.permutation(T)[:S] for _ in range(8)])),
    }


def reference(x_words, x_scales, w1, w2_words, w2_scales, offs):
    xq = unpack_weight(x_words, x_scales)[np.arange(K)[:, None], runs(offs, K)]
    y = mxq(f64(w1), 0, "e4m3").T @ xq
    z = np.maximum(y[:, :V], y[:, V:2 * V])
    return unpack_fp4(w2_words, w2_scales).T @ mxq(z, 0, "e4m3")

@@ -1,0 +1,148 @@
+from contextlib import ExitStack
+
+import concourse.mybir as mybir
+
+K, T, S, H, N, V = 512, 2048, 1024, 512, 128, 512
+FLOPS = 2 * K * H * S + 2 * H * N * V
+
+F32 = mybir.dt.float32
+BF16 = mybir.dt.bfloat16
+I32 = mybir.dt.int32
+U32 = mybir.dt.uint32
+U16 = mybir.dt.uint16
+U8 = mybir.dt.uint8
+FP8X4 = mybir.dt.float8_e4m3fn_x4
+FP4X4 = mybir.dt.float4_e2m1fn_x4
+
+P = 128
+PACK = 4
+QUAD = 32
+PIECE = 256
+CHUNK = 128
+
+
+def tile_picked_phpool_none_p_kernel(
+    tc, x_words, x_scales, w1, w2_words, w2_scales, offs, out
+):
+    nc = tc.nc
+    with ExitStack() as ctx:
+        keep = ctx.enter_context(tc.tile_pool(name="keep", bufs=1))
+        psum = ctx.enter_context(tc.psum_pool(name="psum", bufs=1))
+
+        offsets = keep.tile([P, S // 16], U16, name="offsets")
+        nc.sync.dma_start(offsets[:], offs)
+
+        byte_table = keep.tile([P, T], U8, name="byte_table", tag="shared", align_bytes=64)
+        nc.vector.memset(byte_table[:].bitcast(I32), 0)
+        nc.scalar.dma_start(out=byte_table[0:P:8, :].bitcast(I32), in_=x_scales[0].bitcast(I32))
+
+        w1_raw = keep.tile([P, PACK, H], F32, name="w1_raw")
+        nc.sync.dma_start(out=w1_raw[:], in_=w1.rearrange("(p j) c -> p j c", j=PACK))
+        word_table = keep.tile([P, T], U32, name="word_table")
+        nc.sync.dma_start(
+            out=word_table[:].bitcast(I32),
+            in_=x_words[0].rearrange("p n t -> p (n t)").bitcast(I32),
+        )
+
+        x_plane = keep.tile([P, S], U8, name="x_plane", align_bytes=64)
+        nc.vector.memset(x_plane[:].bitcast(I32), 0)
+        w2_plane = keep.tile([P, N], U8, name="w2_plane", align_bytes=64)
+        nc.vector.memset(w2_plane[:].bitcast(I32), 0)
+        w2_codes = keep.tile([P, 2 * N], U8, name="w2_codes", align_bytes=64)
+        nc.gpsimd.dma_start(out=w2_codes[:].bitcast(I32), in_=w2_words[0].bitcast(I32))
+        for j in range(4):
+            nc.gpsimd.dma_start(
+                out=w2_plane[j:P:QUAD, :].bitcast(I32), in_=w2_scales[0, j:16:4, :].bitcast(I32)
+            )
+
+        picked_bytes = keep.tile([P, S], U8, name="picked_bytes")
+        nc.vector.tensor_copy(picked_bytes[:], byte_table[:].indirect(offsets[:]))
+        for j in range(4):
+            nc.sync.dma_start(
+                out=x_plane[j:P:QUAD, :].bitcast(I32), in_=picked_bytes[8 * j : P : QUAD, :].bitcast(I32)
+            )
+
+        w1_view = w1_raw[:].rearrange("p j (m t) -> p m j t", t=PACK)
+        w1_lo = keep.tile([P, 2, P, PACK], BF16, name="w1_lo", align_bytes=64)
+        nc.scalar.copy(out=w1_lo[:].rearrange("p t m j -> p m j t"), in_=w1_view[:, :, :, 0:2])
+        w1_hi = keep.tile([P, 2, P, PACK], BF16, name="w1_hi", tag="shared", align_bytes=64)
+        nc.vector.tensor_copy(out=w1_hi[:].rearrange("p t m j -> p m j t"), in_=w1_view[:, :, :, 2:4])
+        w1_codes = keep.tile([P, H], U32, name="w1_codes", align_bytes=64)
+        w1_plane = keep.tile([P, H], U8, name="w1_plane", align_bytes=64)
+        for half, grouped in enumerate((w1_lo, w1_hi)):
+            cols = slice(half * 2 * P, (half + 1) * 2 * P)
+            nc.vector.quantize_mx(
+                out=w1_codes[:, cols].bitcast(FP8X4),
+                scales=w1_plane[:, cols],
+                in_=grouped[:].rearrange("p t m j -> p (t m j)"),
+            )
+
+        picked = {}
+        banks = {}
+        for v0 in range(0, V, PIECE):
+            for read in (1, 0):
+                first = read * V + v0
+                words = keep.tile([P, PIECE], U32, name="words_%d" % first, align_bytes=64)
+                nc.vector.tensor_copy(
+                    words[:], word_table[:].indirect(offsets[:, first // 16 : (first + PIECE) // 16])
+                )
+                for c0 in range(0, PIECE, CHUNK):
+                    c = (v0 + c0) // CHUNK
+                    bank = psum.tile([P, PACK, CHUNK], F32, name="y_%d_%d" % (read, c), tag="y_%d_%d" % (read, c))
+                    banks[(read, c)] = bank
+                    for t in range(PACK):
+                        cols = slice(t * P, (t + 1) * P)
+                        nc.tensor.matmul_mx(
+                            out=bank[:, t, :],
+                            lhsT=w1_codes[:, cols].bitcast(FP8X4),
+                            lhsT_scale=w1_plane[:, cols],
+                            rhs=words[:, c0 : c0 + CHUNK].bitcast(FP8X4),
+                            rhs_scale=x_plane[:, first + c0 : first + c0 + CHUNK],
+                            start=True,
+                            stop=True,
+                        )
+                    if read == 1:
+                        second = keep.tile([P, CHUNK, PACK], F32, name="second_%d" % c)
+                        nc.scalar.copy(out=second[:], in_=bank[:].rearrange("p t n -> p n t"))
+                        picked[c] = second
+
+        chunks = V // CHUNK
+        z_tiles = {}
+
+        def larger(c):
+            z = keep.tile([P, CHUNK, PACK], BF16, name="z_%d" % c, align_bytes=64)
+            nc.vector.tensor_tensor(
+                out=z[:],
+                in0=banks[(0, c)][:].rearrange("p t n -> p n t"),
+                in1=picked[c][:],
+                op=mybir.AluOpType.max,
+            )
+            z_tiles[c] = z
+
+        def finish(c):
+            z_codes = keep.tile([P, CHUNK], U32, name="z_codes_%d" % c, align_bytes=64)
+            z_plane = keep.tile([P, CHUNK], U8, name="z_plane_%d" % c, align_bytes=64)
+            nc.vector.quantize_mx(
+                out=z_codes[:].bitcast(FP8X4),
+                scales=z_plane[:],
+                in_=z_tiles[c][:].rearrange("p n t -> p (n t)"),
+            )
+            acc = psum.tile([P, CHUNK], F32, name="acc_%d" % c, tag="y_1_%d" % c)
+            nc.tensor.matmul_mx(
+                out=acc[:],
+                lhsT=w2_codes[:].bitcast(FP4X4),
+                lhsT_scale=w2_plane[:],
+                rhs=z_codes[:].bitcast(FP8X4),
+                rhs_scale=z_plane[:],
+                start=True,
+                stop=True,
+            )
+            result = keep.tile([P, CHUNK], F32, name="result_%d" % c)
+            nc.scalar.copy(out=result[:], in_=acc[:])
+            nc.sync.dma_start(out=out[:, c * CHUNK : (c + 1) * CHUNK], in_=result[:])
+
+        larger(0)
+        for c in range(1, chunks):
+            larger(c)
+            finish(c - 1)
+        finish(chunks - 1)

@@ -36,7 +36,7 @@ def tile_picked_phpool_none_p_kernel(
         nc.vector.memset(byte_table[:].bitcast(I32), 0)
         nc.scalar.dma_start(out=byte_table[0:P:8, :].bitcast(I32), in_=x_scales[0].bitcast(I32))
 
-        w1_raw = keep.tile([P, PACK, H], F32, name="w1_raw")
+        w1_raw = keep.tile([P, PACK, H], F32, name="w1_raw", tag="w1_raw", align_bytes=64)
         nc.sync.dma_start(out=w1_raw[:], in_=w1.rearrange("(p j) c -> p j c", j=PACK))
         word_table = keep.tile([P, T], U32, name="word_table")
         nc.sync.dma_start(
@@ -55,7 +55,7 @@ def tile_picked_phpool_none_p_kernel(
                 out=w2_plane[j:P:QUAD, :].bitcast(I32), in_=w2_scales[0, j:16:4, :].bitcast(I32)
             )
 
-        picked_bytes = keep.tile([P, S], U8, name="picked_bytes")
+        picked_bytes = keep.tile([P, S], U8, name="picked_bytes", tag="picked_bytes", align_bytes=64)
         nc.vector.tensor_copy(picked_bytes[:], byte_table[:].indirect(offsets[:]))
         for j in range(4):
             nc.sync.dma_start(
@@ -63,7 +63,7 @@ def tile_picked_phpool_none_p_kernel(
             )
 
         w1_view = w1_raw[:].rearrange("p j (m t) -> p m j t", t=PACK)
-        w1_lo = keep.tile([P, 2, P, PACK], BF16, name="w1_lo", align_bytes=64)
+        w1_lo = keep.tile([P, 2, P, PACK], BF16, name="w1_lo", tag="w1_lo", align_bytes=64)
         nc.scalar.copy(out=w1_lo[:].rearrange("p t m j -> p m j t"), in_=w1_view[:, :, :, 0:2])
         w1_hi = keep.tile([P, 2, P, PACK], BF16, name="w1_hi", tag="shared", align_bytes=64)
         nc.vector.tensor_copy(out=w1_hi[:].rearrange("p t m j -> p m j t"), in_=w1_view[:, :, :, 2:4])
@@ -77,12 +77,15 @@ def tile_picked_phpool_none_p_kernel(
                 in_=grouped[:].rearrange("p t m j -> p (t m j)"),
             )
 
+        freed = {(1, 0): "w1_lo", (0, 0): "shared", (1, PIECE): "w1_raw", (0, PIECE): "picked_bytes"}
         picked = {}
         banks = {}
         for v0 in range(0, V, PIECE):
             for read in (1, 0):
                 first = read * V + v0
-                words = keep.tile([P, PIECE], U32, name="words_%d" % first, align_bytes=64)
+                words = keep.tile(
+                    [P, PIECE], U32, name="words_%d" % first, tag=freed[(read, v0)], align_bytes=64
+                )
                 nc.vector.tensor_copy(
                     words[:], word_table[:].indirect(offsets[:, first // 16 : (first + PIECE) // 16])
                 )

@@ -33,8 +33,10 @@ def tile_picked_phpool_none_p_kernel(
         nc.sync.dma_start(offsets[:], offs)
 
         byte_table = keep.tile([P, T], U8, name="byte_table", tag="shared", align_bytes=64)
-        nc.vector.memset(byte_table[:].bitcast(I32), 0)
-        nc.scalar.dma_start(out=byte_table[0:P:8, :].bitcast(I32), in_=x_scales[0].bitcast(I32))
+        nc.sync.dma_start(
+            out=byte_table[:].bitcast(I32),
+            in_=x_scales[0].bitcast(I32).unsqueeze(1).to_broadcast([16, 8, T // 4]),
+        )
 
         w1_raw = keep.tile([P, PACK, H], F32, name="w1_raw", tag="w1_raw", align_bytes=64)
         nc.sync.dma_start(out=w1_raw[:], in_=w1.rearrange("(p j) c -> p j c", j=PACK))
@@ -46,14 +48,8 @@ def tile_picked_phpool_none_p_kernel(
 
         x_plane = keep.tile([P, S], U8, name="x_plane", align_bytes=64)
         nc.vector.memset(x_plane[:].bitcast(I32), 0)
-        w2_plane = keep.tile([P, N], U8, name="w2_plane", align_bytes=64)
-        nc.vector.memset(w2_plane[:].bitcast(I32), 0)
         w2_codes = keep.tile([P, 2 * N], U8, name="w2_codes", align_bytes=64)
-        nc.gpsimd.dma_start(out=w2_codes[:].bitcast(I32), in_=w2_words[0].bitcast(I32))
-        for j in range(4):
-            nc.gpsimd.dma_start(
-                out=w2_plane[j:P:QUAD, :].bitcast(I32), in_=w2_scales[0, j:16:4, :].bitcast(I32)
-            )
+        nc.scalar.dma_start(out=w2_codes[:].bitcast(I32), in_=w2_words[0].bitcast(I32))
 
         picked_bytes = keep.tile([P, S], U8, name="picked_bytes", tag="picked_bytes", align_bytes=64)
         nc.vector.tensor_copy(picked_bytes[:], byte_table[:].indirect(offsets[:]))
@@ -62,52 +58,57 @@ def tile_picked_phpool_none_p_kernel(
                 out=x_plane[j:P:QUAD, :].bitcast(I32), in_=picked_bytes[8 * j : P : QUAD, :].bitcast(I32)
             )
 
-        w1_view = w1_raw[:].rearrange("p j (m t) -> p m j t", t=PACK)
-        w1_lo = keep.tile([P, 2, P, PACK], BF16, name="w1_lo", tag="w1_lo", align_bytes=64)
-        nc.scalar.copy(out=w1_lo[:].rearrange("p t m j -> p m j t"), in_=w1_view[:, :, :, 0:2])
-        w1_hi = keep.tile([P, 2, P, PACK], BF16, name="w1_hi", tag="shared", align_bytes=64)
-        nc.vector.tensor_copy(out=w1_hi[:].rearrange("p t m j -> p m j t"), in_=w1_view[:, :, :, 2:4])
-        w1_codes = keep.tile([P, H], U32, name="w1_codes", align_bytes=64)
-        w1_plane = keep.tile([P, H], U8, name="w1_plane", align_bytes=64)
-        for half, grouped in enumerate((w1_lo, w1_hi)):
-            cols = slice(half * 2 * P, (half + 1) * 2 * P)
-            nc.vector.quantize_mx(
-                out=w1_codes[:, cols].bitcast(FP8X4),
-                scales=w1_plane[:, cols],
-                in_=grouped[:].rearrange("p t m j -> p (t m j)"),
+        w2_plane = keep.tile([P, N], U8, name="w2_plane", tag="shared", align_bytes=64)
+        nc.gpsimd.memset(w2_plane[:].bitcast(I32), 0)
+        for j in range(4):
+            nc.sync.dma_start(
+                out=w2_plane[j:P:QUAD, :].bitcast(I32), in_=w2_scales[0, j:16:4, :].bitcast(I32)
             )
 
-        freed = {(1, 0): "w1_lo", (0, 0): "shared", (1, PIECE): "w1_raw", (0, PIECE): "picked_bytes"}
-        picked = {}
-        banks = {}
+        w1_view = w1_raw[:].rearrange("p j (m t) -> p m j t", t=PACK)
+        grouped = keep.tile([P, PACK, P, PACK], BF16, name="grouped", tag="grouped", align_bytes=64)
+        dealt = grouped[:].rearrange("p t m j -> p m j t")
+        nc.scalar.copy(out=dealt[:, :, :, 0:2], in_=w1_view[:, :, :, 0:2])
+        nc.vector.tensor_copy(out=dealt[:, :, :, 2:4], in_=w1_view[:, :, :, 2:4])
+        w1_codes = keep.tile([P, H], U32, name="w1_codes", align_bytes=64)
+        w1_plane = keep.tile([P, H], U8, name="w1_plane", align_bytes=64)
+        nc.vector.quantize_mx(
+            out=w1_codes[:].bitcast(FP8X4),
+            scales=w1_plane[:],
+            in_=grouped[:].rearrange("p t m j -> p (t m j)"),
+        )
+
+        words = keep.tile([P, S], U32, name="words", tag="grouped", align_bytes=64)
         for v0 in range(0, V, PIECE):
             for read in (1, 0):
                 first = read * V + v0
-                words = keep.tile(
-                    [P, PIECE], U32, name="words_%d" % first, tag=freed[(read, v0)], align_bytes=64
-                )
                 nc.vector.tensor_copy(
-                    words[:], word_table[:].indirect(offsets[:, first // 16 : (first + PIECE) // 16])
+                    words[:, first : first + PIECE],
+                    word_table[:].indirect(offsets[:, first // 16 : (first + PIECE) // 16]),
                 )
-                for c0 in range(0, PIECE, CHUNK):
-                    c = (v0 + c0) // CHUNK
-                    bank = psum.tile([P, PACK, CHUNK], F32, name="y_%d_%d" % (read, c), tag="y_%d_%d" % (read, c))
-                    banks[(read, c)] = bank
-                    for t in range(PACK):
-                        cols = slice(t * P, (t + 1) * P)
-                        nc.tensor.matmul_mx(
-                            out=bank[:, t, :],
-                            lhsT=w1_codes[:, cols].bitcast(FP8X4),
-                            lhsT_scale=w1_plane[:, cols],
-                            rhs=words[:, c0 : c0 + CHUNK].bitcast(FP8X4),
-                            rhs_scale=x_plane[:, first + c0 : first + c0 + CHUNK],
-                            start=True,
-                            stop=True,
-                        )
-                    if read == 1:
-                        second = keep.tile([P, CHUNK, PACK], F32, name="second_%d" % c)
-                        nc.scalar.copy(out=second[:], in_=bank[:].rearrange("p t n -> p n t"))
-                        picked[c] = second
+
+        picked = {}
+        banks = {}
+        for c in range(V // CHUNK):
+            for read in (1, 0):
+                entries = slice(read * V + c * CHUNK, read * V + (c + 1) * CHUNK)
+                bank = psum.tile([P, PACK, CHUNK], F32, name="y_%d_%d" % (read, c), tag="y_%d_%d" % (read, c))
+                banks[(read, c)] = bank
+                for t in range(PACK):
+                    cols = slice(t * P, (t + 1) * P)
+                    nc.tensor.matmul_mx(
+                        out=bank[:, t, :],
+                        lhsT=w1_codes[:, cols].bitcast(FP8X4),
+                        lhsT_scale=w1_plane[:, cols],
+                        rhs=words[:, entries].bitcast(FP8X4),
+                        rhs_scale=x_plane[:, entries],
+                        start=True,
+                        stop=True,
+                    )
+                if read == 1:
+                    second = keep.tile([P, CHUNK, PACK], F32, name="second_%d" % c)
+                    nc.scalar.copy(out=second[:], in_=bank[:].rearrange("p t n -> p n t"))
+                    picked[c] = second
 
         chunks = V // CHUNK
         z_tiles = {}

@@ -19,6 +19,7 @@ PACK = 4
 QUAD = 32
 PIECE = 256
 CHUNK = 128
+SCALAR_M = 56
 
 
 def tile_picked_phpool_none_p_kernel(
@@ -33,10 +34,10 @@ def tile_picked_phpool_none_p_kernel(
         nc.sync.dma_start(offsets[:], offs)
 
         byte_table = keep.tile([P, T], U8, name="byte_table", tag="shared", align_bytes=64)
-        nc.sync.dma_start(
-            out=byte_table[:].bitcast(I32),
-            in_=x_scales[0].bitcast(I32).unsqueeze(1).to_broadcast([16, 8, T // 4]),
-        )
+        nc.vector.memset(byte_table[:].bitcast(I32), 0)
+        w2_codes = keep.tile([P, 2 * N], U8, name="w2_codes", align_bytes=64)
+        nc.sync.dma_start(out=w2_codes[:].bitcast(I32), in_=w2_words[0].bitcast(I32))
+        nc.sync.dma_start(out=byte_table[0:P:8, :].bitcast(I32), in_=x_scales[0].bitcast(I32))
 
         w1_raw = keep.tile([P, PACK, H], F32, name="w1_raw", tag="w1_raw", align_bytes=64)
         nc.sync.dma_start(out=w1_raw[:], in_=w1.rearrange("(p j) c -> p j c", j=PACK))
@@ -48,8 +49,6 @@ def tile_picked_phpool_none_p_kernel(
 
         x_plane = keep.tile([P, S], U8, name="x_plane", align_bytes=64)
         nc.vector.memset(x_plane[:].bitcast(I32), 0)
-        w2_codes = keep.tile([P, 2 * N], U8, name="w2_codes", align_bytes=64)
-        nc.scalar.dma_start(out=w2_codes[:].bitcast(I32), in_=w2_words[0].bitcast(I32))
 
         picked_bytes = keep.tile([P, S], U8, name="picked_bytes", tag="picked_bytes", align_bytes=64)
         nc.vector.tensor_copy(picked_bytes[:], byte_table[:].indirect(offsets[:]))
@@ -58,18 +57,18 @@ def tile_picked_phpool_none_p_kernel(
                 out=x_plane[j:P:QUAD, :].bitcast(I32), in_=picked_bytes[8 * j : P : QUAD, :].bitcast(I32)
             )
 
-        w2_plane = keep.tile([P, N], U8, name="w2_plane", tag="shared", align_bytes=64)
+        w2_plane = keep.tile([P, N], U8, name="w2_plane", tag="picked_bytes", align_bytes=64)
         nc.gpsimd.memset(w2_plane[:].bitcast(I32), 0)
         for j in range(4):
             nc.sync.dma_start(
                 out=w2_plane[j:P:QUAD, :].bitcast(I32), in_=w2_scales[0, j:16:4, :].bitcast(I32)
             )
 
-        w1_view = w1_raw[:].rearrange("p j (m t) -> p m j t", t=PACK)
+        w1_view = w1_raw[:].rearrange("p j (m t) -> p m t j", t=PACK)
         grouped = keep.tile([P, PACK, P, PACK], BF16, name="grouped", tag="grouped", align_bytes=64)
-        dealt = grouped[:].rearrange("p t m j -> p m j t")
-        nc.scalar.copy(out=dealt[:, :, :, 0:2], in_=w1_view[:, :, :, 0:2])
-        nc.vector.tensor_copy(out=dealt[:, :, :, 2:4], in_=w1_view[:, :, :, 2:4])
+        dealt = grouped[:].rearrange("p t m j -> p m t j")
+        nc.scalar.copy(out=dealt[:, 0:SCALAR_M], in_=w1_view[:, 0:SCALAR_M])
+        nc.vector.tensor_copy(out=dealt[:, SCALAR_M:P], in_=w1_view[:, SCALAR_M:P])
         w1_codes = keep.tile([P, H], U32, name="w1_codes", align_bytes=64)
         w1_plane = keep.tile([P, H], U8, name="w1_plane", align_bytes=64)
         nc.vector.quantize_mx(

@@ -77,6 +77,18 @@ def tile_picked_phpool_none_p_kernel(
             in_=grouped[:].rearrange("p t m j -> p (t m j)"),
         )
 
+        warm = psum.tile([P, H], F32, name="warm", tag="y_0_%d" % (V // CHUNK - 1))
+        for t in range(2):
+            nc.tensor.matmul_mx(
+                out=warm[:],
+                lhsT=w1_codes[:, 0:P].bitcast(FP8X4),
+                lhsT_scale=w1_plane[:, 0:P],
+                rhs=w1_codes[:].bitcast(FP8X4),
+                rhs_scale=w1_plane[:],
+                start=True,
+                stop=True,
+            )
+
         words = keep.tile([P, S], U32, name="words", tag="grouped", align_bytes=64)
         for v0 in range(0, V, PIECE):
             for read in (1, 0):

@@ -19,7 +19,7 @@ PACK = 4
 QUAD = 32
 PIECE = 256
 CHUNK = 128
-SCALAR_M = 56
+SCALAR_M = 108
 
 
 def tile_picked_phpool_none_p_kernel(
@@ -35,17 +35,25 @@ def tile_picked_phpool_none_p_kernel(
 
         byte_table = keep.tile([P, T], U8, name="byte_table", tag="shared", align_bytes=64)
         nc.vector.memset(byte_table[:].bitcast(I32), 0)
-        w2_codes = keep.tile([P, 2 * N], U8, name="w2_codes", align_bytes=64)
-        nc.sync.dma_start(out=w2_codes[:].bitcast(I32), in_=w2_words[0].bitcast(I32))
-        nc.sync.dma_start(out=byte_table[0:P:8, :].bitcast(I32), in_=x_scales[0].bitcast(I32))
+        w1_rows = w1.rearrange("(p j) c -> p j c", j=PACK)
 
-        w1_raw = keep.tile([P, PACK, H], F32, name="w1_raw", tag="w1_raw", align_bytes=64)
-        nc.sync.dma_start(out=w1_raw[:], in_=w1.rearrange("(p j) c -> p j c", j=PACK))
+        def load_w1(first, last):
+            part = keep.tile([P, PACK, last - first], F32, name="w1_raw_%d" % first, align_bytes=64)
+            nc.sync.dma_start(out=part[:], in_=w1_rows[:, :, first:last])
+            return part[:].rearrange("p j (m t) -> p m t j", t=PACK)
+
+        w1_first = load_w1(0, H // 4)
+        nc.sync.dma_start(out=byte_table[0:P:8, :].bitcast(I32), in_=x_scales[0].bitcast(I32))
+        w1_second = load_w1(H // 4, H // 2)
+        w1_rest = load_w1(H // 2, H)
         word_table = keep.tile([P, T], U32, name="word_table")
         nc.sync.dma_start(
             out=word_table[:].bitcast(I32),
             in_=x_words[0].rearrange("p n t -> p (n t)").bitcast(I32),
         )
+
+        w2_codes = keep.tile([P, 2 * N], U8, name="w2_codes", align_bytes=64)
+        nc.sync.dma_start(out=w2_codes[:].bitcast(I32), in_=w2_words[0].bitcast(I32))
 
         x_plane = keep.tile([P, S], U8, name="x_plane", align_bytes=64)
         nc.vector.memset(x_plane[:].bitcast(I32), 0)
@@ -64,11 +72,12 @@ def tile_picked_phpool_none_p_kernel(
                 out=w2_plane[j:P:QUAD, :].bitcast(I32), in_=w2_scales[0, j:16:4, :].bitcast(I32)
             )
 
-        w1_view = w1_raw[:].rearrange("p j (m t) -> p m t j", t=PACK)
         grouped = keep.tile([P, PACK, P, PACK], BF16, name="grouped", tag="grouped", align_bytes=64)
         dealt = grouped[:].rearrange("p t m j -> p m t j")
-        nc.scalar.copy(out=dealt[:, 0:SCALAR_M], in_=w1_view[:, 0:SCALAR_M])
-        nc.vector.tensor_copy(out=dealt[:, SCALAR_M:P], in_=w1_view[:, SCALAR_M:P])
+        nc.scalar.copy(out=dealt[:, 0 : P // 4], in_=w1_first)
+        nc.scalar.copy(out=dealt[:, P // 4 : P // 2], in_=w1_second)
+        nc.scalar.copy(out=dealt[:, P // 2 : SCALAR_M], in_=w1_rest[:, 0 : SCALAR_M - P // 2])
+        nc.vector.tensor_copy(out=dealt[:, SCALAR_M:P], in_=w1_rest[:, SCALAR_M - P // 2 : P // 2])
         w1_codes = keep.tile([P, H], U32, name="w1_codes", align_bytes=64)
         w1_plane = keep.tile([P, H], U8, name="w1_plane", align_bytes=64)
         nc.vector.quantize_mx(
@@ -99,12 +108,10 @@ def tile_picked_phpool_none_p_kernel(
                 )
 
         picked = {}
-        banks = {}
         for c in range(V // CHUNK):
             for read in (1, 0):
                 entries = slice(read * V + c * CHUNK, read * V + (c + 1) * CHUNK)
                 bank = psum.tile([P, PACK, CHUNK], F32, name="y_%d_%d" % (read, c), tag="y_%d_%d" % (read, c))
-                banks[(read, c)] = bank
                 for t in range(PACK):
                     cols = slice(t * P, (t + 1) * P)
                     nc.tensor.matmul_mx(
@@ -116,10 +123,13 @@ def tile_picked_phpool_none_p_kernel(
                         start=True,
                         stop=True,
                     )
-                if read == 1:
-                    second = keep.tile([P, CHUNK, PACK], F32, name="second_%d" % c)
-                    nc.scalar.copy(out=second[:], in_=bank[:].rearrange("p t n -> p n t"))
-                    picked[c] = second
+                last = c == V // CHUNK - 1
+                if read == 1 or last:
+                    copied = keep.tile([P, CHUNK, PACK], BF16 if last else F32, name="copied_%d_%d" % (read, c))
+                    nc.scalar.copy(out=copied[:], in_=bank[:].rearrange("p t n -> p n t"))
+                    picked[(read, c)] = copied[:]
+                else:
+                    picked[(read, c)] = bank[:].rearrange("p t n -> p n t")
 
         chunks = V // CHUNK
         z_tiles = {}
@@ -128,8 +138,8 @@ def tile_picked_phpool_none_p_kernel(
             z = keep.tile([P, CHUNK, PACK], BF16, name="z_%d" % c, align_bytes=64)
             nc.vector.tensor_tensor(
                 out=z[:],
-                in0=banks[(0, c)][:].rearrange("p t n -> p n t"),
-                in1=picked[c][:],
+                in0=picked[(0, c)],
+                in1=picked[(1, c)],
                 op=mybir.AluOpType.max,
             )
             z_tiles[c] = z

@@ -19,7 +19,7 @@ PACK = 4
 QUAD = 32
 PIECE = 256
 CHUNK = 128
-SCALAR_M = 108
+SCALAR_M = 64
 
 
 def tile_picked_phpool_none_p_kernel(
@@ -37,15 +37,10 @@ def tile_picked_phpool_none_p_kernel(
         nc.vector.memset(byte_table[:].bitcast(I32), 0)
         w1_rows = w1.rearrange("(p j) c -> p j c", j=PACK)
 
-        def load_w1(first, last):
-            part = keep.tile([P, PACK, last - first], F32, name="w1_raw_%d" % first, align_bytes=64)
-            nc.sync.dma_start(out=part[:], in_=w1_rows[:, :, first:last])
-            return part[:].rearrange("p j (m t) -> p m t j", t=PACK)
-
-        w1_first = load_w1(0, H // 4)
+        w1_raw = keep.tile([P, PACK, H], F32, name="w1_raw", align_bytes=64)
+        nc.sync.dma_start(out=w1_raw[:, 0, :], in_=w1_rows[:, 0, :])
         nc.sync.dma_start(out=byte_table[0:P:8, :].bitcast(I32), in_=x_scales[0].bitcast(I32))
-        w1_second = load_w1(H // 4, H // 2)
-        w1_rest = load_w1(H // 2, H)
+        nc.sync.dma_start(out=w1_raw[:, 1:PACK, :], in_=w1_rows[:, 1:PACK, :])
         word_table = keep.tile([P, T], U32, name="word_table")
         nc.sync.dma_start(
             out=word_table[:].bitcast(I32),
@@ -57,6 +52,9 @@ def tile_picked_phpool_none_p_kernel(
 
         x_plane = keep.tile([P, S], U8, name="x_plane", align_bytes=64)
         nc.vector.memset(x_plane[:].bitcast(I32), 0)
+
+        unread = keep.tile([P, 1], U32, name="unread")
+        nc.scalar.copy(out=unread[:], in_=x_plane[:, 0:4].bitcast(U32))
 
         picked_bytes = keep.tile([P, S], U8, name="picked_bytes", tag="picked_bytes", align_bytes=64)
         nc.vector.tensor_copy(picked_bytes[:], byte_table[:].indirect(offsets[:]))
@@ -74,26 +72,27 @@ def tile_picked_phpool_none_p_kernel(
 
         grouped = keep.tile([P, PACK, P, PACK], BF16, name="grouped", tag="grouped", align_bytes=64)
         dealt = grouped[:].rearrange("p t m j -> p m t j")
-        nc.scalar.copy(out=dealt[:, 0 : P // 4], in_=w1_first)
-        nc.scalar.copy(out=dealt[:, P // 4 : P // 2], in_=w1_second)
-        nc.scalar.copy(out=dealt[:, P // 2 : SCALAR_M], in_=w1_rest[:, 0 : SCALAR_M - P // 2])
-        nc.vector.tensor_copy(out=dealt[:, SCALAR_M:P], in_=w1_rest[:, SCALAR_M - P // 2 : P // 2])
+        w1_view = w1_raw[:].rearrange("p j (m t) -> p m t j", t=PACK)
+        nc.scalar.copy(out=dealt[:, 0:SCALAR_M], in_=w1_view[:, 0:SCALAR_M])
+        nc.vector.tensor_copy(out=dealt[:, SCALAR_M:P], in_=w1_view[:, SCALAR_M:P])
         w1_codes = keep.tile([P, H], U32, name="w1_codes", align_bytes=64)
         w1_plane = keep.tile([P, H], U8, name="w1_plane", align_bytes=64)
-        nc.vector.quantize_mx(
-            out=w1_codes[:].bitcast(FP8X4),
-            scales=w1_plane[:],
-            in_=grouped[:].rearrange("p t m j -> p (t m j)"),
-        )
+        for t in range(PACK):
+            cols = slice(t * P, (t + 1) * P)
+            nc.vector.quantize_mx(
+                out=w1_codes[:, cols].bitcast(FP8X4),
+                scales=w1_plane[:, cols],
+                in_=grouped[:, t].rearrange("p m j -> p (m j)"),
+            )
 
         warm = psum.tile([P, H], F32, name="warm", tag="y_0_%d" % (V // CHUNK - 1))
-        for t in range(2):
+        for width in (H // 2, H, H // 2):
             nc.tensor.matmul_mx(
-                out=warm[:],
+                out=warm[:, 0:width],
                 lhsT=w1_codes[:, 0:P].bitcast(FP8X4),
                 lhsT_scale=w1_plane[:, 0:P],
-                rhs=w1_codes[:].bitcast(FP8X4),
-                rhs_scale=w1_plane[:],
+                rhs=w1_codes[:, 0:width].bitcast(FP8X4),
+                rhs_scale=w1_plane[:, 0:width],
                 start=True,
                 stop=True,
             )
@@ -108,8 +107,10 @@ def tile_picked_phpool_none_p_kernel(
                 )
 
         picked = {}
-        for c in range(V // CHUNK):
-            for read in (1, 0):
+        for step in range(V // CHUNK + 1):
+            for read, c in ((1, step), (0, step - 1)):
+                if not 0 <= c < V // CHUNK:
+                    continue
                 entries = slice(read * V + c * CHUNK, read * V + (c + 1) * CHUNK)
                 bank = psum.tile([P, PACK, CHUNK], F32, name="y_%d_%d" % (read, c), tag="y_%d_%d" % (read, c))
                 for t in range(PACK):

@@ -17,9 +17,13 @@ FP4X4 = mybir.dt.float4_e2m1fn_x4
 P = 128
 PACK = 4
 QUAD = 32
+BLOCK = 8
 PIECE = 256
 CHUNK = 128
-SCALAR_M = 64
+CHUNKS = V // CHUNK
+LEAD_ROWS = 2
+LEAD_BANKS = 2
+SCALAR_GROUPS = 100
 
 
 def tile_picked_phpool_none_p_kernel(
@@ -31,61 +35,67 @@ def tile_picked_phpool_none_p_kernel(
         psum = ctx.enter_context(tc.psum_pool(name="psum", bufs=1))
 
         offsets = keep.tile([P, S // 16], U16, name="offsets")
-        nc.sync.dma_start(offsets[:], offs)
-
-        byte_table = keep.tile([P, T], U8, name="byte_table", tag="shared", align_bytes=64)
+        byte_table = keep.tile([P, T], U8, name="byte_table", align_bytes=64)
         nc.vector.memset(byte_table[:].bitcast(I32), 0)
         w1_rows = w1.rearrange("(p j) c -> p j c", j=PACK)
-
-        w1_raw = keep.tile([P, PACK, H], F32, name="w1_raw", align_bytes=64)
-        nc.sync.dma_start(out=w1_raw[:, 0, :], in_=w1_rows[:, 0, :])
-        nc.sync.dma_start(out=byte_table[0:P:8, :].bitcast(I32), in_=x_scales[0].bitcast(I32))
-        nc.sync.dma_start(out=w1_raw[:, 1:PACK, :], in_=w1_rows[:, 1:PACK, :])
+        low = keep.tile([P, PACK, H // 2], F32, name="w1_low", align_bytes=64)
+        high = keep.tile([P, PACK, H // 2], F32, name="w1_high", tag="w1_high", align_bytes=64)
+        nc.sync.dma_start(out=low[:, 0:LEAD_ROWS, :], in_=w1_rows[:, 0:LEAD_ROWS, 0 : H // 2])
+        nc.sync.dma_start(offsets[:], offs)
+        nc.sync.dma_start(out=byte_table[0:P:BLOCK, :].bitcast(I32), in_=x_scales[0].bitcast(I32))
+        nc.sync.dma_start(out=low[:, LEAD_ROWS:PACK, :], in_=w1_rows[:, LEAD_ROWS:PACK, 0 : H // 2])
+        nc.sync.dma_start(out=high[:], in_=w1_rows[:, :, H // 2 : H])
         word_table = keep.tile([P, T], U32, name="word_table")
         nc.sync.dma_start(
             out=word_table[:].bitcast(I32),
             in_=x_words[0].rearrange("p n t -> p (n t)").bitcast(I32),
         )
 
-        w2_codes = keep.tile([P, 2 * N], U8, name="w2_codes", align_bytes=64)
-        nc.sync.dma_start(out=w2_codes[:].bitcast(I32), in_=w2_words[0].bitcast(I32))
-
-        x_plane = keep.tile([P, S], U8, name="x_plane", align_bytes=64)
-        nc.vector.memset(x_plane[:].bitcast(I32), 0)
+        x_planes = [keep.tile([P, V], U8, name="x_plane_%d" % read, align_bytes=64) for read in range(2)]
+        for plane in x_planes:
+            nc.vector.memset(plane[:].bitcast(I32), 0)
 
         unread = keep.tile([P, 1], U32, name="unread")
-        nc.scalar.copy(out=unread[:], in_=x_plane[:, 0:4].bitcast(U32))
+        nc.scalar.copy(out=unread[:], in_=x_planes[0][:, 0:PACK].bitcast(U32))
 
-        picked_bytes = keep.tile([P, S], U8, name="picked_bytes", tag="picked_bytes", align_bytes=64)
-        nc.vector.tensor_copy(picked_bytes[:], byte_table[:].indirect(offsets[:]))
-        for j in range(4):
-            nc.sync.dma_start(
-                out=x_plane[j:P:QUAD, :].bitcast(I32), in_=picked_bytes[8 * j : P : QUAD, :].bitcast(I32)
+        for read in (1, 0):
+            picked_bytes = keep.tile([P, V], U8, name="picked_bytes_%d" % read, tag="picked_%d" % read, align_bytes=64)
+            nc.vector.tensor_copy(
+                picked_bytes[:], byte_table[:].indirect(offsets[:, read * V // 16 : (read + 1) * V // 16])
             )
+            for j in range(PACK):
+                nc.sync.dma_start(
+                    out=x_planes[read][j:P:QUAD, :].bitcast(I32),
+                    in_=picked_bytes[BLOCK * j : P : QUAD, :].bitcast(I32),
+                )
 
-        w2_plane = keep.tile([P, N], U8, name="w2_plane", tag="picked_bytes", align_bytes=64)
-        nc.gpsimd.memset(w2_plane[:].bitcast(I32), 0)
-        for j in range(4):
-            nc.sync.dma_start(
-                out=w2_plane[j:P:QUAD, :].bitcast(I32), in_=w2_scales[0, j:16:4, :].bitcast(I32)
-            )
-
-        grouped = keep.tile([P, PACK, P, PACK], BF16, name="grouped", tag="grouped", align_bytes=64)
+        grouped = keep.tile([P, PACK, P, PACK], BF16, name="grouped", align_bytes=64)
         dealt = grouped[:].rearrange("p t m j -> p m t j")
-        w1_view = w1_raw[:].rearrange("p j (m t) -> p m t j", t=PACK)
-        nc.scalar.copy(out=dealt[:, 0:SCALAR_M], in_=w1_view[:, 0:SCALAR_M])
-        nc.vector.tensor_copy(out=dealt[:, SCALAR_M:P], in_=w1_view[:, SCALAR_M:P])
+        high_view = high[:].rearrange("p j (m t) -> p m t j", t=PACK)
+        nc.scalar.copy(out=dealt[:, 0 : P // 2], in_=low[:].rearrange("p j (m t) -> p m t j", t=PACK))
+        nc.scalar.copy(out=dealt[:, P // 2 : SCALAR_GROUPS], in_=high_view[:, 0 : SCALAR_GROUPS - P // 2])
+        nc.vector.tensor_copy(out=dealt[:, SCALAR_GROUPS:P], in_=high_view[:, SCALAR_GROUPS - P // 2 : P // 2])
+
+        w2_plane = keep.tile([P, N], U8, name="w2_plane", tag="w1_high", align_bytes=64)
+        nc.vector.memset(w2_plane[:].bitcast(I32), 0)
+        for j in range(PACK):
+            nc.sync.dma_start(
+                out=w2_plane[j:P:QUAD, :].bitcast(I32), in_=w2_scales[0, j : H // QUAD : PACK, :].bitcast(I32)
+            )
+        w2_codes = keep.tile([P, 2 * N], U8, name="w2_codes", tag="picked_1", align_bytes=64)
+        nc.sync.dma_start(out=w2_codes[:].bitcast(I32), in_=w2_words[0].bitcast(I32))
+
         w1_codes = keep.tile([P, H], U32, name="w1_codes", align_bytes=64)
         w1_plane = keep.tile([P, H], U8, name="w1_plane", align_bytes=64)
-        for t in range(PACK):
-            cols = slice(t * P, (t + 1) * P)
+        for t in range(0, PACK, 2):
+            cols = slice(t * P, (t + 2) * P)
             nc.vector.quantize_mx(
                 out=w1_codes[:, cols].bitcast(FP8X4),
                 scales=w1_plane[:, cols],
-                in_=grouped[:, t].rearrange("p m j -> p (m j)"),
+                in_=grouped[:, t : t + 2].rearrange("p t m j -> p (t m j)"),
             )
 
-        warm = psum.tile([P, H], F32, name="warm", tag="y_0_%d" % (V // CHUNK - 1))
+        warm = psum.tile([P, H], F32, name="warm", tag="y_0_%d" % (CHUNKS - 1))
         for width in (H // 2, H, H // 2):
             nc.tensor.matmul_mx(
                 out=warm[:, 0:width],
@@ -97,21 +107,19 @@ def tile_picked_phpool_none_p_kernel(
                 stop=True,
             )
 
-        words = keep.tile([P, S], U32, name="words", tag="grouped", align_bytes=64)
-        for v0 in range(0, V, PIECE):
-            for read in (1, 0):
-                first = read * V + v0
+        words = keep.tile([P, S], U32, name="words", align_bytes=64)
+        for read in (1, 0):
+            for first in range(read * V, (read + 1) * V, PIECE):
                 nc.vector.tensor_copy(
                     words[:, first : first + PIECE],
                     word_table[:].indirect(offsets[:, first // 16 : (first + PIECE) // 16]),
                 )
 
-        picked = {}
-        for step in range(V // CHUNK + 1):
-            for read, c in ((1, step), (0, step - 1)):
-                if not 0 <= c < V // CHUNK:
+        y = {}
+        for step in range(CHUNKS + LEAD_BANKS):
+            for read, c in ((1, step), (0, step - LEAD_BANKS)):
+                if not 0 <= c < CHUNKS:
                     continue
-                entries = slice(read * V + c * CHUNK, read * V + (c + 1) * CHUNK)
                 bank = psum.tile([P, PACK, CHUNK], F32, name="y_%d_%d" % (read, c), tag="y_%d_%d" % (read, c))
                 for t in range(PACK):
                     cols = slice(t * P, (t + 1) * P)
@@ -119,30 +127,25 @@ def tile_picked_phpool_none_p_kernel(
                         out=bank[:, t, :],
                         lhsT=w1_codes[:, cols].bitcast(FP8X4),
                         lhsT_scale=w1_plane[:, cols],
-                        rhs=words[:, entries].bitcast(FP8X4),
-                        rhs_scale=x_plane[:, entries],
+                        rhs=words[:, read * V + c * CHUNK : read * V + (c + 1) * CHUNK].bitcast(FP8X4),
+                        rhs_scale=x_planes[read][:, c * CHUNK : (c + 1) * CHUNK],
                         start=True,
                         stop=True,
                     )
-                last = c == V // CHUNK - 1
+                interleaved = bank[:].rearrange("p t n -> p n t")
+                last = c == CHUNKS - 1
                 if read == 1 or last:
                     copied = keep.tile([P, CHUNK, PACK], BF16 if last else F32, name="copied_%d_%d" % (read, c))
-                    nc.scalar.copy(out=copied[:], in_=bank[:].rearrange("p t n -> p n t"))
-                    picked[(read, c)] = copied[:]
+                    nc.scalar.copy(out=copied[:], in_=interleaved)
+                    y[(read, c)] = copied[:]
                 else:
-                    picked[(read, c)] = bank[:].rearrange("p t n -> p n t")
+                    y[(read, c)] = interleaved
 
-        chunks = V // CHUNK
         z_tiles = {}
 
         def larger(c):
             z = keep.tile([P, CHUNK, PACK], BF16, name="z_%d" % c, align_bytes=64)
-            nc.vector.tensor_tensor(
-                out=z[:],
-                in0=picked[(0, c)],
-                in1=picked[(1, c)],
-                op=mybir.AluOpType.max,
-            )
+            nc.vector.tensor_tensor(out=z[:], in0=y[(0, c)], in1=y[(1, c)], op=mybir.AluOpType.max)
             z_tiles[c] = z
 
         def finish(c):
@@ -164,11 +167,14 @@ def tile_picked_phpool_none_p_kernel(
                 stop=True,
             )
             result = keep.tile([P, CHUNK], F32, name="result_%d" % c)
-            nc.scalar.copy(out=result[:], in_=acc[:])
+            if c == CHUNKS - 1:
+                nc.vector.tensor_copy(out=result[:], in_=acc[:])
+            else:
+                nc.scalar.copy(out=result[:], in_=acc[:])
             nc.sync.dma_start(out=out[:, c * CHUNK : (c + 1) * CHUNK], in_=result[:])
 
         larger(0)
-        for c in range(1, chunks):
+        for c in range(1, CHUNKS):
             larger(c)
             finish(c - 1)
-        finish(chunks - 1)
+        finish(CHUNKS - 1)

@@ -21,9 +21,10 @@ BLOCK = 8
 PIECE = 256
 CHUNK = 128
 CHUNKS = V // CHUNK
-LEAD_ROWS = 2
+LEAD_ROWS = 1
 LEAD_BANKS = 2
-SCALAR_GROUPS = 100
+EARLY = V
+SCALAR_GROUPS = 64
 
 
 def tile_picked_phpool_none_p_kernel(
@@ -38,103 +39,111 @@ def tile_picked_phpool_none_p_kernel(
         byte_table = keep.tile([P, T], U8, name="byte_table", align_bytes=64)
         nc.vector.memset(byte_table[:].bitcast(I32), 0)
         w1_rows = w1.rearrange("(p j) c -> p j c", j=PACK)
-        low = keep.tile([P, PACK, H // 2], F32, name="w1_low", align_bytes=64)
-        high = keep.tile([P, PACK, H // 2], F32, name="w1_high", tag="w1_high", align_bytes=64)
-        nc.sync.dma_start(out=low[:, 0:LEAD_ROWS, :], in_=w1_rows[:, 0:LEAD_ROWS, 0 : H // 2])
+        w1_raw = keep.tile([P, PACK, H], F32, name="w1_raw", tag="w1_raw", align_bytes=64)
+        nc.sync.dma_start(out=w1_raw[:, 0:LEAD_ROWS, :], in_=w1_rows[:, 0:LEAD_ROWS, :])
         nc.sync.dma_start(offsets[:], offs)
         nc.sync.dma_start(out=byte_table[0:P:BLOCK, :].bitcast(I32), in_=x_scales[0].bitcast(I32))
-        nc.sync.dma_start(out=low[:, LEAD_ROWS:PACK, :], in_=w1_rows[:, LEAD_ROWS:PACK, 0 : H // 2])
-        nc.sync.dma_start(out=high[:], in_=w1_rows[:, :, H // 2 : H])
+        nc.sync.dma_start(out=w1_raw[:, LEAD_ROWS:PACK, :], in_=w1_rows[:, LEAD_ROWS:PACK, :])
         word_table = keep.tile([P, T], U32, name="word_table")
         nc.sync.dma_start(
             out=word_table[:].bitcast(I32),
             in_=x_words[0].rearrange("p n t -> p (n t)").bitcast(I32),
         )
 
-        x_planes = [keep.tile([P, V], U8, name="x_plane_%d" % read, align_bytes=64) for read in range(2)]
+        spans = ((0, EARLY), (EARLY, S))
+        x_planes = [keep.tile([P, b - a], U8, name="x_plane_%d" % a, align_bytes=64) for a, b in spans]
         for plane in x_planes:
             nc.vector.memset(plane[:].bitcast(I32), 0)
+
+        idle = keep.tile([P, (PACK + 2) * H], U8, name="idle", align_bytes=64)
+        nc.vector.memset(idle[:].bitcast(I32), 0)
+        idle_codes = idle[:, 0 : PACK * H].bitcast(U32)
+        idle_plane = idle[:, PACK * H : (PACK + 1) * H]
+        nc.vector.quantize_mx(
+            out=idle_codes[:, 0 : P // 2].bitcast(FP8X4),
+            scales=idle_plane[:, 0 : P // 2],
+            in_=idle[:, (PACK + 1) * H : (PACK + 2) * H].bitcast(BF16),
+        )
 
         unread = keep.tile([P, 1], U32, name="unread")
         nc.scalar.copy(out=unread[:], in_=x_planes[0][:, 0:PACK].bitcast(U32))
 
-        for read in (1, 0):
-            picked_bytes = keep.tile([P, V], U8, name="picked_bytes_%d" % read, tag="picked_%d" % read, align_bytes=64)
-            nc.vector.tensor_copy(
-                picked_bytes[:], byte_table[:].indirect(offsets[:, read * V // 16 : (read + 1) * V // 16])
-            )
+        picked = []
+        for (a, b), plane in zip(spans, x_planes):
+            picked_bytes = keep.tile([P, b - a], U8, name="picked_bytes_%d" % a, tag="picked_%d" % a, align_bytes=64)
+            nc.vector.tensor_copy(picked_bytes[:], byte_table[:].indirect(offsets[:, a // 16 : b // 16]))
+            picked.append(picked_bytes)
             for j in range(PACK):
                 nc.sync.dma_start(
-                    out=x_planes[read][j:P:QUAD, :].bitcast(I32),
+                    out=plane[j:P:QUAD, :].bitcast(I32),
                     in_=picked_bytes[BLOCK * j : P : QUAD, :].bitcast(I32),
                 )
 
+        warm = psum.tile([P, H], F32, name="warm", tag="y_1_%d" % (CHUNKS - 1))
+        for width in (H, H, P):
+            nc.tensor.matmul_mx(
+                out=warm[:, 0:width],
+                lhsT=idle_codes[:, 0:P].bitcast(FP8X4),
+                lhsT_scale=picked[1][:, 0:P],
+                rhs=idle_codes[:, 0:width].bitcast(FP8X4),
+                rhs_scale=idle_plane[:, 0:width],
+                start=True,
+                stop=True,
+            )
+
         grouped = keep.tile([P, PACK, P, PACK], BF16, name="grouped", align_bytes=64)
         dealt = grouped[:].rearrange("p t m j -> p m t j")
-        high_view = high[:].rearrange("p j (m t) -> p m t j", t=PACK)
-        nc.scalar.copy(out=dealt[:, 0 : P // 2], in_=low[:].rearrange("p j (m t) -> p m t j", t=PACK))
-        nc.scalar.copy(out=dealt[:, P // 2 : SCALAR_GROUPS], in_=high_view[:, 0 : SCALAR_GROUPS - P // 2])
-        nc.vector.tensor_copy(out=dealt[:, SCALAR_GROUPS:P], in_=high_view[:, SCALAR_GROUPS - P // 2 : P // 2])
+        source = w1_raw[:].rearrange("p j (m t) -> p m t j", t=PACK)
+        nc.scalar.copy(out=dealt[:, 0:SCALAR_GROUPS], in_=source[:, 0:SCALAR_GROUPS])
+        nc.vector.tensor_copy(out=dealt[:, SCALAR_GROUPS:P], in_=source[:, SCALAR_GROUPS:P])
 
-        w2_plane = keep.tile([P, N], U8, name="w2_plane", tag="w1_high", align_bytes=64)
+        w2_plane = keep.tile([P, N], U8, name="w2_plane", tag="w1_raw", align_bytes=64)
         nc.vector.memset(w2_plane[:].bitcast(I32), 0)
         for j in range(PACK):
             nc.sync.dma_start(
                 out=w2_plane[j:P:QUAD, :].bitcast(I32), in_=w2_scales[0, j : H // QUAD : PACK, :].bitcast(I32)
             )
-        w2_codes = keep.tile([P, 2 * N], U8, name="w2_codes", tag="picked_1", align_bytes=64)
+        w2_codes = keep.tile([P, 2 * N], U8, name="w2_codes", tag="picked_0", align_bytes=64)
         nc.sync.dma_start(out=w2_codes[:].bitcast(I32), in_=w2_words[0].bitcast(I32))
 
         w1_codes = keep.tile([P, H], U32, name="w1_codes", align_bytes=64)
         w1_plane = keep.tile([P, H], U8, name="w1_plane", align_bytes=64)
-        for t in range(0, PACK, 2):
-            cols = slice(t * P, (t + 2) * P)
-            nc.vector.quantize_mx(
-                out=w1_codes[:, cols].bitcast(FP8X4),
-                scales=w1_plane[:, cols],
-                in_=grouped[:, t : t + 2].rearrange("p t m j -> p (t m j)"),
-            )
-
-        warm = psum.tile([P, H], F32, name="warm", tag="y_0_%d" % (CHUNKS - 1))
-        for width in (H // 2, H, H // 2):
-            nc.tensor.matmul_mx(
-                out=warm[:, 0:width],
-                lhsT=w1_codes[:, 0:P].bitcast(FP8X4),
-                lhsT_scale=w1_plane[:, 0:P],
-                rhs=w1_codes[:, 0:width].bitcast(FP8X4),
-                rhs_scale=w1_plane[:, 0:width],
-                start=True,
-                stop=True,
-            )
+        nc.vector.quantize_mx(
+            out=w1_codes[:].bitcast(FP8X4),
+            scales=w1_plane[:],
+            in_=grouped[:].rearrange("p t m j -> p (t m j)"),
+        )
 
         words = keep.tile([P, S], U32, name="words", align_bytes=64)
-        for read in (1, 0):
-            for first in range(read * V, (read + 1) * V, PIECE):
-                nc.vector.tensor_copy(
-                    words[:, first : first + PIECE],
-                    word_table[:].indirect(offsets[:, first // 16 : (first + PIECE) // 16]),
-                )
+        for first in range(0, S, PIECE):
+            nc.vector.tensor_copy(
+                words[:, first : first + PIECE],
+                word_table[:].indirect(offsets[:, first // 16 : (first + PIECE) // 16]),
+            )
 
         y = {}
         for step in range(CHUNKS + LEAD_BANKS):
-            for read, c in ((1, step), (0, step - LEAD_BANKS)):
+            for read, c in ((0, step), (1, step - LEAD_BANKS)):
                 if not 0 <= c < CHUNKS:
                     continue
                 bank = psum.tile([P, PACK, CHUNK], F32, name="y_%d_%d" % (read, c), tag="y_%d_%d" % (read, c))
+                first = read * V + c * CHUNK
+                late = int(first >= EARLY)
+                in_plane = first - late * EARLY
                 for t in range(PACK):
                     cols = slice(t * P, (t + 1) * P)
                     nc.tensor.matmul_mx(
                         out=bank[:, t, :],
                         lhsT=w1_codes[:, cols].bitcast(FP8X4),
                         lhsT_scale=w1_plane[:, cols],
-                        rhs=words[:, read * V + c * CHUNK : read * V + (c + 1) * CHUNK].bitcast(FP8X4),
-                        rhs_scale=x_planes[read][:, c * CHUNK : (c + 1) * CHUNK],
+                        rhs=words[:, first : first + CHUNK].bitcast(FP8X4),
+                        rhs_scale=x_planes[late][:, in_plane : in_plane + CHUNK],
                         start=True,
                         stop=True,
                     )
                 interleaved = bank[:].rearrange("p t n -> p n t")
                 last = c == CHUNKS - 1
-                if read == 1 or last:
+                if read == 0 or last:
                     copied = keep.tile([P, CHUNK, PACK], BF16 if last else F32, name="copied_%d_%d" % (read, c))
                     nc.scalar.copy(out=copied[:], in_=interleaved)
                     y[(read, c)] = copied[:]
@@ -145,7 +154,7 @@ def tile_picked_phpool_none_p_kernel(
 
         def larger(c):
             z = keep.tile([P, CHUNK, PACK], BF16, name="z_%d" % c, align_bytes=64)
-            nc.vector.tensor_tensor(out=z[:], in0=y[(0, c)], in1=y[(1, c)], op=mybir.AluOpType.max)
+            nc.vector.tensor_tensor(out=z[:], in0=y[(1, c)], in1=y[(0, c)], op=mybir.AluOpType.max)
             z_tiles[c] = z
 
         def finish(c):
@@ -156,7 +165,7 @@ def tile_picked_phpool_none_p_kernel(
                 scales=z_plane[:],
                 in_=z_tiles[c][:].rearrange("p n t -> p (n t)"),
             )
-            acc = psum.tile([P, CHUNK], F32, name="acc_%d" % c, tag="y_1_%d" % c)
+            acc = psum.tile([P, CHUNK], F32, name="acc_%d" % c, tag="y_0_%d" % c)
             nc.tensor.matmul_mx(
                 out=acc[:],
                 lhsT=w2_codes[:].bitcast(FP4X4),

@@ -24,7 +24,7 @@ CHUNKS = V // CHUNK
 LEAD_ROWS = 1
 LEAD_BANKS = 2
 EARLY = V
-SCALAR_GROUPS = 64
+SCALAR_GROUPS = 56
 
 
 def tile_picked_phpool_none_p_kernel(
@@ -45,10 +45,11 @@ def tile_picked_phpool_none_p_kernel(
         nc.sync.dma_start(out=byte_table[0:P:BLOCK, :].bitcast(I32), in_=x_scales[0].bitcast(I32))
         nc.sync.dma_start(out=w1_raw[:, LEAD_ROWS:PACK, :], in_=w1_rows[:, LEAD_ROWS:PACK, :])
         word_table = keep.tile([P, T], U32, name="word_table")
-        nc.sync.dma_start(
-            out=word_table[:].bitcast(I32),
-            in_=x_words[0].rearrange("p n t -> p (n t)").bitcast(I32),
-        )
+        x_rows = x_words[0].rearrange("p n t -> p (n t)").bitcast(I32)
+        w2_codes = keep.tile([P, 2 * N], U8, name="w2_codes", align_bytes=64)
+        nc.sync.dma_start(out=word_table[:, 0 : T // 2].bitcast(I32), in_=x_rows[:, 0 : T // 2])
+        nc.sync.dma_start(out=w2_codes[:].bitcast(I32), in_=w2_words[0].bitcast(I32))
+        nc.sync.dma_start(out=word_table[:, T // 2 : T].bitcast(I32), in_=x_rows[:, T // 2 : T])
 
         spans = ((0, EARLY), (EARLY, S))
         x_planes = [keep.tile([P, b - a], U8, name="x_plane_%d" % a, align_bytes=64) for a, b in spans]
@@ -68,11 +69,9 @@ def tile_picked_phpool_none_p_kernel(
         unread = keep.tile([P, 1], U32, name="unread")
         nc.scalar.copy(out=unread[:], in_=x_planes[0][:, 0:PACK].bitcast(U32))
 
-        picked = []
         for (a, b), plane in zip(spans, x_planes):
             picked_bytes = keep.tile([P, b - a], U8, name="picked_bytes_%d" % a, tag="picked_%d" % a, align_bytes=64)
             nc.vector.tensor_copy(picked_bytes[:], byte_table[:].indirect(offsets[:, a // 16 : b // 16]))
-            picked.append(picked_bytes)
             for j in range(PACK):
                 nc.sync.dma_start(
                     out=plane[j:P:QUAD, :].bitcast(I32),
@@ -83,8 +82,8 @@ def tile_picked_phpool_none_p_kernel(
         for width in (H, H, P):
             nc.tensor.matmul_mx(
                 out=warm[:, 0:width],
-                lhsT=idle_codes[:, 0:P].bitcast(FP8X4),
-                lhsT_scale=picked[1][:, 0:P],
+                lhsT=w2_codes[:].bitcast(FP4X4),
+                lhsT_scale=idle_plane[:, 0:N],
                 rhs=idle_codes[:, 0:width].bitcast(FP8X4),
                 rhs_scale=idle_plane[:, 0:width],
                 start=True,
@@ -103,8 +102,6 @@ def tile_picked_phpool_none_p_kernel(
             nc.sync.dma_start(
                 out=w2_plane[j:P:QUAD, :].bitcast(I32), in_=w2_scales[0, j : H // QUAD : PACK, :].bitcast(I32)
             )
-        w2_codes = keep.tile([P, 2 * N], U8, name="w2_codes", tag="picked_0", align_bytes=64)
-        nc.sync.dma_start(out=w2_codes[:].bitcast(I32), in_=w2_words[0].bitcast(I32))
 
         w1_codes = keep.tile([P, H], U32, name="w1_codes", align_bytes=64)
         w1_plane = keep.tile([P, H], U8, name="w1_plane", align_bytes=64)

@@ -21,10 +21,11 @@ BLOCK = 8
 PIECE = 256
 CHUNK = 128
 CHUNKS = V // CHUNK
-LEAD_ROWS = 1
+W1_LEAD = 320
 LEAD_BANKS = 2
 EARLY = V
-SCALAR_GROUPS = 56
+SCALAR_GROUPS = 48
+X_LEAD = 5 * T // 8
 
 
 def tile_picked_phpool_none_p_kernel(
@@ -38,18 +39,25 @@ def tile_picked_phpool_none_p_kernel(
         offsets = keep.tile([P, S // 16], U16, name="offsets")
         byte_table = keep.tile([P, T], U8, name="byte_table", align_bytes=64)
         nc.vector.memset(byte_table[:].bitcast(I32), 0)
-        w1_rows = w1.rearrange("(p j) c -> p j c", j=PACK)
-        w1_raw = keep.tile([P, PACK, H], F32, name="w1_raw", tag="w1_raw", align_bytes=64)
-        nc.sync.dma_start(out=w1_raw[:, 0:LEAD_ROWS, :], in_=w1_rows[:, 0:LEAD_ROWS, :])
+        w1_rows = w1.rearrange("(p j) c -> p (j c)", j=PACK)
+        w1_raw = keep.tile([P, PACK * H], F32, name="w1_raw", align_bytes=64)
+        nc.sync.dma_start(out=w1_raw[:, 0:W1_LEAD], in_=w1_rows[:, 0:W1_LEAD])
         nc.sync.dma_start(offsets[:], offs)
         nc.sync.dma_start(out=byte_table[0:P:BLOCK, :].bitcast(I32), in_=x_scales[0].bitcast(I32))
-        nc.sync.dma_start(out=w1_raw[:, LEAD_ROWS:PACK, :], in_=w1_rows[:, LEAD_ROWS:PACK, :])
+        nc.sync.dma_start(out=w1_raw[:, W1_LEAD : PACK * H], in_=w1_rows[:, W1_LEAD : PACK * H])
         word_table = keep.tile([P, T], U32, name="word_table")
         x_rows = x_words[0].rearrange("p n t -> p (n t)").bitcast(I32)
-        w2_codes = keep.tile([P, 2 * N], U8, name="w2_codes", align_bytes=64)
-        nc.sync.dma_start(out=word_table[:, 0 : T // 2].bitcast(I32), in_=x_rows[:, 0 : T // 2])
-        nc.sync.dma_start(out=w2_codes[:].bitcast(I32), in_=w2_words[0].bitcast(I32))
-        nc.sync.dma_start(out=word_table[:, T // 2 : T].bitcast(I32), in_=x_rows[:, T // 2 : T])
+        w2_plane = keep.tile([P, N], U8, name="w2_plane", align_bytes=64)
+        nc.vector.memset(w2_plane[:].bitcast(I32), 0)
+
+        def load_w2_scales(j):
+            nc.sync.dma_start(
+                out=w2_plane[j:P:QUAD, :].bitcast(I32), in_=w2_scales[0, j : H // QUAD : PACK, :].bitcast(I32)
+            )
+
+        nc.sync.dma_start(out=word_table[:, 0:X_LEAD].bitcast(I32), in_=x_rows[:, 0:X_LEAD])
+        load_w2_scales(0)
+        nc.sync.dma_start(out=word_table[:, X_LEAD:T].bitcast(I32), in_=x_rows[:, X_LEAD:T])
 
         spans = ((0, EARLY), (EARLY, S))
         x_planes = [keep.tile([P, b - a], U8, name="x_plane_%d" % a, align_bytes=64) for a, b in spans]
@@ -82,8 +90,8 @@ def tile_picked_phpool_none_p_kernel(
         for width in (H, H, P):
             nc.tensor.matmul_mx(
                 out=warm[:, 0:width],
-                lhsT=w2_codes[:].bitcast(FP4X4),
-                lhsT_scale=idle_plane[:, 0:N],
+                lhsT=idle_codes[:, 0:P].bitcast(FP8X4),
+                lhsT_scale=w2_plane[:],
                 rhs=idle_codes[:, 0:width].bitcast(FP8X4),
                 rhs_scale=idle_plane[:, 0:width],
                 start=True,
@@ -92,16 +100,14 @@ def tile_picked_phpool_none_p_kernel(
 
         grouped = keep.tile([P, PACK, P, PACK], BF16, name="grouped", align_bytes=64)
         dealt = grouped[:].rearrange("p t m j -> p m t j")
-        source = w1_raw[:].rearrange("p j (m t) -> p m t j", t=PACK)
+        source = w1_raw[:].rearrange("p (j m t) -> p m t j", j=PACK, t=PACK)
         nc.scalar.copy(out=dealt[:, 0:SCALAR_GROUPS], in_=source[:, 0:SCALAR_GROUPS])
         nc.vector.tensor_copy(out=dealt[:, SCALAR_GROUPS:P], in_=source[:, SCALAR_GROUPS:P])
 
-        w2_plane = keep.tile([P, N], U8, name="w2_plane", tag="w1_raw", align_bytes=64)
-        nc.vector.memset(w2_plane[:].bitcast(I32), 0)
-        for j in range(PACK):
-            nc.sync.dma_start(
-                out=w2_plane[j:P:QUAD, :].bitcast(I32), in_=w2_scales[0, j : H // QUAD : PACK, :].bitcast(I32)
-            )
+        for j in range(1, PACK):
+            load_w2_scales(j)
+        w2_codes = keep.tile([P, 2 * N], U8, name="w2_codes", tag="picked_0", align_bytes=64)
+        nc.sync.dma_start(out=w2_codes[:].bitcast(I32), in_=w2_words[0].bitcast(I32))
 
         w1_codes = keep.tile([P, H], U32, name="w1_codes", align_bytes=64)
         w1_plane = keep.tile([P, H], U8, name="w1_plane", align_bytes=64)

@@ -25,7 +25,9 @@ W1_LEAD = 320
 LEAD_BANKS = 2
 EARLY = V
 SCALAR_GROUPS = 48
-X_LEAD = 5 * T // 8
+WARM_PASSES = 3
+WARM_ROWS = 64
+X_LEAD = 7 * T // 16
 
 
 def tile_picked_phpool_none_p_kernel(
@@ -87,13 +89,13 @@ def tile_picked_phpool_none_p_kernel(
                 )
 
         warm = psum.tile([P, H], F32, name="warm", tag="y_1_%d" % (CHUNKS - 1))
-        for width in (H, H, P):
+        for turn in range(WARM_PASSES):
             nc.tensor.matmul_mx(
-                out=warm[:, 0:width],
-                lhsT=idle_codes[:, 0:P].bitcast(FP8X4),
-                lhsT_scale=w2_plane[:],
-                rhs=idle_codes[:, 0:width].bitcast(FP8X4),
-                rhs_scale=idle_plane[:, 0:width],
+                out=warm[0:WARM_ROWS, :],
+                lhsT=idle_codes[:, 0:WARM_ROWS].bitcast(FP8X4),
+                lhsT_scale=w2_plane[:, 0:WARM_ROWS],
+                rhs=idle_codes.bitcast(FP8X4),
+                rhs_scale=idle_plane,
                 start=True,
                 stop=True,
             )

@@ -18,16 +18,18 @@ P = 128
 PACK = 4
 QUAD = 32
 BLOCK = 8
+GROUP = 16
 PIECE = 256
 CHUNK = 128
 CHUNKS = V // CHUNK
-W1_LEAD = 320
 LEAD_BANKS = 2
-EARLY = V
-SCALAR_GROUPS = 48
+W1_LEAD = 320
+SCALAR_GROUPS = 56
+X_LEAD = 7 * T // 16
 WARM_PASSES = 3
 WARM_ROWS = 64
-X_LEAD = 7 * T // 16
+
+assert PACK * SCALAR_GROUPS <= W1_LEAD <= H
 
 
 def tile_picked_phpool_none_p_kernel(
@@ -38,7 +40,7 @@ def tile_picked_phpool_none_p_kernel(
         keep = ctx.enter_context(tc.tile_pool(name="keep", bufs=1))
         psum = ctx.enter_context(tc.psum_pool(name="psum", bufs=1))
 
-        offsets = keep.tile([P, S // 16], U16, name="offsets")
+        offsets = keep.tile([P, S // GROUP], U16, name="offsets")
         byte_table = keep.tile([P, T], U8, name="byte_table", align_bytes=64)
         nc.vector.memset(byte_table[:].bitcast(I32), 0)
         w1_rows = w1.rearrange("(p j) c -> p (j c)", j=PACK)
@@ -47,6 +49,7 @@ def tile_picked_phpool_none_p_kernel(
         nc.sync.dma_start(offsets[:], offs)
         nc.sync.dma_start(out=byte_table[0:P:BLOCK, :].bitcast(I32), in_=x_scales[0].bitcast(I32))
         nc.sync.dma_start(out=w1_raw[:, W1_LEAD : PACK * H], in_=w1_rows[:, W1_LEAD : PACK * H])
+
         word_table = keep.tile([P, T], U32, name="word_table")
         x_rows = x_words[0].rearrange("p n t -> p (n t)").bitcast(I32)
         w2_plane = keep.tile([P, N], U8, name="w2_plane", align_bytes=64)
@@ -61,8 +64,7 @@ def tile_picked_phpool_none_p_kernel(
         load_w2_scales(0)
         nc.sync.dma_start(out=word_table[:, X_LEAD:T].bitcast(I32), in_=x_rows[:, X_LEAD:T])
 
-        spans = ((0, EARLY), (EARLY, S))
-        x_planes = [keep.tile([P, b - a], U8, name="x_plane_%d" % a, align_bytes=64) for a, b in spans]
+        x_planes = [keep.tile([P, V], U8, name="x_plane_%d" % read, align_bytes=64) for read in range(2)]
         for plane in x_planes:
             nc.vector.memset(plane[:].bitcast(I32), 0)
 
@@ -70,21 +72,20 @@ def tile_picked_phpool_none_p_kernel(
         nc.vector.memset(idle[:].bitcast(I32), 0)
         idle_codes = idle[:, 0 : PACK * H].bitcast(U32)
         idle_plane = idle[:, PACK * H : (PACK + 1) * H]
+        idle_values = idle[:, (PACK + 1) * H : (PACK + 2) * H].bitcast(BF16)
+        idle_columns = H // 2 // PACK
         nc.vector.quantize_mx(
-            out=idle_codes[:, 0 : P // 2].bitcast(FP8X4),
-            scales=idle_plane[:, 0 : P // 2],
-            in_=idle[:, (PACK + 1) * H : (PACK + 2) * H].bitcast(BF16),
+            out=idle_codes[:, 0:idle_columns].bitcast(FP8X4), scales=idle_plane[:, 0:idle_columns], in_=idle_values
         )
 
-        unread = keep.tile([P, 1], U32, name="unread")
-        nc.scalar.copy(out=unread[:], in_=x_planes[0][:, 0:PACK].bitcast(U32))
-
-        for (a, b), plane in zip(spans, x_planes):
-            picked_bytes = keep.tile([P, b - a], U8, name="picked_bytes_%d" % a, tag="picked_%d" % a, align_bytes=64)
-            nc.vector.tensor_copy(picked_bytes[:], byte_table[:].indirect(offsets[:, a // 16 : b // 16]))
+        for read in range(2):
+            picked_bytes = keep.tile([P, V], U8, name="picked_bytes_%d" % read, tag="picked_%d" % read, align_bytes=64)
+            nc.vector.tensor_copy(
+                picked_bytes[:], byte_table[:].indirect(offsets[:, read * V // GROUP : (read + 1) * V // GROUP])
+            )
             for j in range(PACK):
                 nc.sync.dma_start(
-                    out=plane[j:P:QUAD, :].bitcast(I32),
+                    out=x_planes[read][j:P:QUAD, :].bitcast(I32),
                     in_=picked_bytes[BLOCK * j : P : QUAD, :].bitcast(I32),
                 )
 
@@ -103,7 +104,8 @@ def tile_picked_phpool_none_p_kernel(
         grouped = keep.tile([P, PACK, P, PACK], BF16, name="grouped", align_bytes=64)
         dealt = grouped[:].rearrange("p t m j -> p m t j")
         source = w1_raw[:].rearrange("p (j m t) -> p m t j", j=PACK, t=PACK)
-        nc.scalar.copy(out=dealt[:, 0:SCALAR_GROUPS], in_=source[:, 0:SCALAR_GROUPS])
+        nc.scalar.copy(out=dealt[:, 0:SCALAR_GROUPS, :, 0], in_=source[:, 0:SCALAR_GROUPS, :, 0])
+        nc.scalar.copy(out=dealt[:, 0:SCALAR_GROUPS, :, 1:PACK], in_=source[:, 0:SCALAR_GROUPS, :, 1:PACK])
         nc.vector.tensor_copy(out=dealt[:, SCALAR_GROUPS:P], in_=source[:, SCALAR_GROUPS:P])
 
         for j in range(1, PACK):
@@ -123,7 +125,7 @@ def tile_picked_phpool_none_p_kernel(
         for first in range(0, S, PIECE):
             nc.vector.tensor_copy(
                 words[:, first : first + PIECE],
-                word_table[:].indirect(offsets[:, first // 16 : (first + PIECE) // 16]),
+                word_table[:].indirect(offsets[:, first // GROUP : (first + PIECE) // GROUP]),
             )
 
         y = {}
@@ -132,17 +134,15 @@ def tile_picked_phpool_none_p_kernel(
                 if not 0 <= c < CHUNKS:
                     continue
                 bank = psum.tile([P, PACK, CHUNK], F32, name="y_%d_%d" % (read, c), tag="y_%d_%d" % (read, c))
-                first = read * V + c * CHUNK
-                late = int(first >= EARLY)
-                in_plane = first - late * EARLY
+                entry = read * V + c * CHUNK
                 for t in range(PACK):
                     cols = slice(t * P, (t + 1) * P)
                     nc.tensor.matmul_mx(
                         out=bank[:, t, :],
                         lhsT=w1_codes[:, cols].bitcast(FP8X4),
                         lhsT_scale=w1_plane[:, cols],
-                        rhs=words[:, first : first + CHUNK].bitcast(FP8X4),
-                        rhs_scale=x_planes[late][:, in_plane : in_plane + CHUNK],
+                        rhs=words[:, entry : entry + CHUNK].bitcast(FP8X4),
+                        rhs_scale=x_planes[read][:, c * CHUNK : (c + 1) * CHUNK],
                         start=True,
                         stop=True,
                     )

@@ -26,8 +26,6 @@ LEAD_BANKS = 2
 W1_LEAD = 320
 SCALAR_GROUPS = 56
 X_LEAD = 7 * T // 16
-WARM_PASSES = 3
-WARM_ROWS = 64
 
 assert PACK * SCALAR_GROUPS <= W1_LEAD <= H
 
@@ -68,16 +66,6 @@ def tile_picked_phpool_none_p_kernel(
         for plane in x_planes:
             nc.vector.memset(plane[:].bitcast(I32), 0)
 
-        idle = keep.tile([P, (PACK + 2) * H], U8, name="idle", align_bytes=64)
-        nc.vector.memset(idle[:].bitcast(I32), 0)
-        idle_codes = idle[:, 0 : PACK * H].bitcast(U32)
-        idle_plane = idle[:, PACK * H : (PACK + 1) * H]
-        idle_values = idle[:, (PACK + 1) * H : (PACK + 2) * H].bitcast(BF16)
-        idle_columns = H // 2 // PACK
-        nc.vector.quantize_mx(
-            out=idle_codes[:, 0:idle_columns].bitcast(FP8X4), scales=idle_plane[:, 0:idle_columns], in_=idle_values
-        )
-
         for read in range(2):
             picked_bytes = keep.tile([P, V], U8, name="picked_bytes_%d" % read, tag="picked_%d" % read, align_bytes=64)
             nc.vector.tensor_copy(
@@ -88,18 +76,6 @@ def tile_picked_phpool_none_p_kernel(
                     out=x_planes[read][j:P:QUAD, :].bitcast(I32),
                     in_=picked_bytes[BLOCK * j : P : QUAD, :].bitcast(I32),
                 )
-
-        warm = psum.tile([P, H], F32, name="warm", tag="y_1_%d" % (CHUNKS - 1))
-        for turn in range(WARM_PASSES):
-            nc.tensor.matmul_mx(
-                out=warm[0:WARM_ROWS, :],
-                lhsT=idle_codes[:, 0:WARM_ROWS].bitcast(FP8X4),
-                lhsT_scale=w2_plane[:, 0:WARM_ROWS],
-                rhs=idle_codes.bitcast(FP8X4),
-                rhs_scale=idle_plane,
-                start=True,
-                stop=True,
-            )
 
         grouped = keep.tile([P, PACK, P, PACK], BF16, name="grouped", align_bytes=64)
         dealt = grouped[:].rearrange("p t m j -> p m t j")

@@ -25,7 +25,8 @@ CHUNKS = V // CHUNK
 LEAD_BANKS = 2
 W1_LEAD = 320
 SCALAR_GROUPS = 56
-X_LEAD = 7 * T // 16
+EARLY = 768
+BOTH = 2
 
 assert PACK * SCALAR_GROUPS <= W1_LEAD <= H
 
@@ -39,43 +40,29 @@ def tile_picked_phpool_none_p_kernel(
         psum = ctx.enter_context(tc.psum_pool(name="psum", bufs=1))
 
         offsets = keep.tile([P, S // GROUP], U16, name="offsets")
-        byte_table = keep.tile([P, T], U8, name="byte_table", align_bytes=64)
+        byte_table = keep.tile([P, T], U8, name="byte_table", tag="table", align_bytes=64)
         nc.vector.memset(byte_table[:].bitcast(I32), 0)
         w1_rows = w1.rearrange("(p j) c -> p (j c)", j=PACK)
-        w1_raw = keep.tile([P, PACK * H], F32, name="w1_raw", align_bytes=64)
+        w1_raw = keep.tile([P, PACK * H], F32, name="w1_raw", tag="raw", align_bytes=64)
         nc.sync.dma_start(out=w1_raw[:, 0:W1_LEAD], in_=w1_rows[:, 0:W1_LEAD])
         nc.sync.dma_start(offsets[:], offs)
         nc.sync.dma_start(out=byte_table[0:P:BLOCK, :].bitcast(I32), in_=x_scales[0].bitcast(I32))
         nc.sync.dma_start(out=w1_raw[:, W1_LEAD : PACK * H], in_=w1_rows[:, W1_LEAD : PACK * H])
-
         word_table = keep.tile([P, T], U32, name="word_table")
-        x_rows = x_words[0].rearrange("p n t -> p (n t)").bitcast(I32)
-        w2_plane = keep.tile([P, N], U8, name="w2_plane", align_bytes=64)
-        nc.vector.memset(w2_plane[:].bitcast(I32), 0)
+        nc.sync.dma_start(out=word_table[:].bitcast(I32), in_=x_words[0].rearrange("p n t -> p (n t)").bitcast(I32))
 
-        def load_w2_scales(j):
-            nc.sync.dma_start(
-                out=w2_plane[j:P:QUAD, :].bitcast(I32), in_=w2_scales[0, j : H // QUAD : PACK, :].bitcast(I32)
-            )
-
-        nc.sync.dma_start(out=word_table[:, 0:X_LEAD].bitcast(I32), in_=x_rows[:, 0:X_LEAD])
-        load_w2_scales(0)
-        nc.sync.dma_start(out=word_table[:, X_LEAD:T].bitcast(I32), in_=x_rows[:, X_LEAD:T])
-
-        x_planes = [keep.tile([P, V], U8, name="x_plane_%d" % read, align_bytes=64) for read in range(2)]
-        for plane in x_planes:
+        def pick_scales(first, last, tag):
+            plane = keep.tile([P, last - first], U8, name="x_plane_%d" % first, align_bytes=64)
             nc.vector.memset(plane[:].bitcast(I32), 0)
-
-        for read in range(2):
-            picked_bytes = keep.tile([P, V], U8, name="picked_bytes_%d" % read, tag="picked_%d" % read, align_bytes=64)
-            nc.vector.tensor_copy(
-                picked_bytes[:], byte_table[:].indirect(offsets[:, read * V // GROUP : (read + 1) * V // GROUP])
-            )
+            picked = keep.tile([P, last - first], U8, name="picked_%d" % first, tag=tag, align_bytes=64)
+            nc.vector.tensor_copy(picked[:], byte_table[:].indirect(offsets[:, first // GROUP : last // GROUP]))
             for j in range(PACK):
                 nc.sync.dma_start(
-                    out=x_planes[read][j:P:QUAD, :].bitcast(I32),
-                    in_=picked_bytes[BLOCK * j : P : QUAD, :].bitcast(I32),
+                    out=plane[j:P:QUAD, :].bitcast(I32), in_=picked[BLOCK * j : P : QUAD, :].bitcast(I32)
                 )
+            return plane
+
+        early_plane = pick_scales(0, EARLY, "picked")
 
         grouped = keep.tile([P, PACK, P, PACK], BF16, name="grouped", align_bytes=64)
         dealt = grouped[:].rearrange("p t m j -> p m t j")
@@ -84,25 +71,50 @@ def tile_picked_phpool_none_p_kernel(
         nc.scalar.copy(out=dealt[:, 0:SCALAR_GROUPS, :, 1:PACK], in_=source[:, 0:SCALAR_GROUPS, :, 1:PACK])
         nc.vector.tensor_copy(out=dealt[:, SCALAR_GROUPS:P], in_=source[:, SCALAR_GROUPS:P])
 
-        for j in range(1, PACK):
-            load_w2_scales(j)
-        w2_codes = keep.tile([P, 2 * N], U8, name="w2_codes", tag="picked_0", align_bytes=64)
-        nc.sync.dma_start(out=w2_codes[:].bitcast(I32), in_=w2_words[0].bitcast(I32))
-
         w1_codes = keep.tile([P, H], U32, name="w1_codes", align_bytes=64)
         w1_plane = keep.tile([P, H], U8, name="w1_plane", align_bytes=64)
-        nc.vector.quantize_mx(
-            out=w1_codes[:].bitcast(FP8X4),
-            scales=w1_plane[:],
-            in_=grouped[:].rearrange("p t m j -> p (t m j)"),
-        )
-
-        words = keep.tile([P, S], U32, name="words", align_bytes=64)
-        for first in range(0, S, PIECE):
-            nc.vector.tensor_copy(
-                words[:, first : first + PIECE],
-                word_table[:].indirect(offsets[:, first // GROUP : (first + PIECE) // GROUP]),
+        for first in range(0, PACK, 2):
+            cols = slice(first * P, (first + 2) * P)
+            nc.vector.quantize_mx(
+                out=w1_codes[:, cols].bitcast(FP8X4),
+                scales=w1_plane[:, cols],
+                in_=grouped[:, first : first + 2].rearrange("p t m j -> p (t m j)"),
             )
+
+        warm = psum.tile([P, H], F32, name="warm", tag="y_1_%d" % (CHUNKS - 1))
+        for rows, columns in ((128, 256), (64, 512), (64, 512),):
+            nc.tensor.matmul_mx(
+                out=warm[0:rows, 0:columns],
+                lhsT=w1_codes[:, 0:rows].bitcast(FP8X4),
+                lhsT_scale=w1_plane[:, 0:rows],
+                rhs=w1_codes[:, 0:columns].bitcast(FP8X4),
+                rhs_scale=w1_plane[:, 0:columns],
+                start=True,
+                stop=True,
+            )
+
+        late_plane = pick_scales(EARLY, S, "raw")
+
+        w2_plane = keep.tile([P, N], U8, name="w2_plane", tag="table", align_bytes=64)
+        for j in range(PACK):
+            nc.sync.dma_start(
+                out=w2_plane[j:P:QUAD, :].bitcast(I32), in_=w2_scales[0, j : H // QUAD : PACK, :].bitcast(I32)
+            )
+        w2_codes = keep.tile([P, 2 * N], U8, name="w2_codes", tag="picked", align_bytes=64)
+        nc.sync.dma_start(out=w2_codes[:].bitcast(I32), in_=w2_words[0].bitcast(I32))
+
+        def x_scale(entry):
+            if entry < EARLY:
+                return early_plane[:, entry : entry + CHUNK]
+            return late_plane[:, entry - EARLY : entry - EARLY + CHUNK]
+
+        words = []
+        for first in range(0, S, PIECE):
+            piece = keep.tile([P, PIECE], U32, name="words_%d" % first, tag="words_%d" % first, align_bytes=64)
+            nc.vector.tensor_copy(
+                piece[:], word_table[:].indirect(offsets[:, first // GROUP : (first + PIECE) // GROUP])
+            )
+            words.append(piece)
 
         y = {}
         for step in range(CHUNKS + LEAD_BANKS):
@@ -111,21 +123,22 @@ def tile_picked_phpool_none_p_kernel(
                     continue
                 bank = psum.tile([P, PACK, CHUNK], F32, name="y_%d_%d" % (read, c), tag="y_%d_%d" % (read, c))
                 entry = read * V + c * CHUNK
+                within = entry % PIECE
                 for t in range(PACK):
                     cols = slice(t * P, (t + 1) * P)
                     nc.tensor.matmul_mx(
                         out=bank[:, t, :],
                         lhsT=w1_codes[:, cols].bitcast(FP8X4),
                         lhsT_scale=w1_plane[:, cols],
-                        rhs=words[:, entry : entry + CHUNK].bitcast(FP8X4),
-                        rhs_scale=x_planes[read][:, c * CHUNK : (c + 1) * CHUNK],
+                        rhs=words[entry // PIECE][:, within : within + CHUNK].bitcast(FP8X4),
+                        rhs_scale=x_scale(entry),
                         start=True,
                         stop=True,
                     )
                 interleaved = bank[:].rearrange("p t n -> p n t")
-                last = c == CHUNKS - 1
-                if read == 0 or last:
-                    copied = keep.tile([P, CHUNK, PACK], BF16 if last else F32, name="copied_%d_%d" % (read, c))
+                both = c == BOTH
+                if read == 0 or both:
+                    copied = keep.tile([P, CHUNK, PACK], BF16 if both else F32, name="copied_%d_%d" % (read, c))
                     nc.scalar.copy(out=copied[:], in_=interleaved)
                     y[(read, c)] = copied[:]
                 else:
@@ -138,15 +151,15 @@ def tile_picked_phpool_none_p_kernel(
             nc.vector.tensor_tensor(out=z[:], in0=y[(1, c)], in1=y[(0, c)], op=mybir.AluOpType.max)
             z_tiles[c] = z
 
-        def finish(c):
-            z_codes = keep.tile([P, CHUNK], U32, name="z_codes_%d" % c, align_bytes=64)
+        def finish(c, slot, bank):
+            z_codes = keep.tile([P, CHUNK], U32, name="z_codes_%d" % c, tag=slot, align_bytes=64)
             z_plane = keep.tile([P, CHUNK], U8, name="z_plane_%d" % c, align_bytes=64)
             nc.vector.quantize_mx(
                 out=z_codes[:].bitcast(FP8X4),
                 scales=z_plane[:],
                 in_=z_tiles[c][:].rearrange("p n t -> p (n t)"),
             )
-            acc = psum.tile([P, CHUNK], F32, name="acc_%d" % c, tag="y_0_%d" % c)
+            acc = psum.tile([P, CHUNK], F32, name="acc_%d" % c, tag=bank)
             nc.tensor.matmul_mx(
                 out=acc[:],
                 lhsT=w2_codes[:].bitcast(FP4X4),
@@ -157,14 +170,17 @@ def tile_picked_phpool_none_p_kernel(
                 stop=True,
             )
             result = keep.tile([P, CHUNK], F32, name="result_%d" % c)
-            if c == CHUNKS - 1:
+            if c == BOTH:
                 nc.vector.tensor_copy(out=result[:], in_=acc[:])
             else:
                 nc.scalar.copy(out=result[:], in_=acc[:])
             nc.sync.dma_start(out=out[:, c * CHUNK : (c + 1) * CHUNK], in_=result[:])
 
         larger(0)
-        for c in range(1, CHUNKS):
-            larger(c)
-            finish(c - 1)
-        finish(CHUNKS - 1)
+        larger(1)
+        finish(0, "words_0", "y_1_%d" % BOTH)
+        larger(3)
+        finish(1, "words_%d" % (S - PIECE), "y_0_0")
+        larger(BOTH)
+        finish(3, "words_%d" % PIECE, "y_0_1")
+        finish(BOTH, "words_%d" % (2 * PIECE), "y_0_2")

@@ -24,11 +24,11 @@ CHUNK = 128
 CHUNKS = V // CHUNK
 LEAD_BANKS = 2
 W1_LEAD = 320
-SCALAR_GROUPS = 56
+VECTOR_GROUPS = 80
 EARLY = 768
 BOTH = 2
 
-assert PACK * SCALAR_GROUPS <= W1_LEAD <= H
+assert W1_LEAD <= PACK * VECTOR_GROUPS
 
 
 def tile_picked_phpool_none_p_kernel(
@@ -37,13 +37,14 @@ def tile_picked_phpool_none_p_kernel(
     nc = tc.nc
     with ExitStack() as ctx:
         keep = ctx.enter_context(tc.tile_pool(name="keep", bufs=1))
+        reused = ctx.enter_context(tc.tile_pool(name="reused", bufs=1))
         psum = ctx.enter_context(tc.psum_pool(name="psum", bufs=1))
 
         offsets = keep.tile([P, S // GROUP], U16, name="offsets")
         byte_table = keep.tile([P, T], U8, name="byte_table", tag="table", align_bytes=64)
         nc.vector.memset(byte_table[:].bitcast(I32), 0)
         w1_rows = w1.rearrange("(p j) c -> p (j c)", j=PACK)
-        w1_raw = keep.tile([P, PACK * H], F32, name="w1_raw", tag="raw", align_bytes=64)
+        w1_raw = reused.tile([P, PACK * H], F32, name="w1_raw", offset=0, align_bytes=64)
         nc.sync.dma_start(out=w1_raw[:, 0:W1_LEAD], in_=w1_rows[:, 0:W1_LEAD])
         nc.sync.dma_start(offsets[:], offs)
         nc.sync.dma_start(out=byte_table[0:P:BLOCK, :].bitcast(I32), in_=x_scales[0].bitcast(I32))
@@ -51,10 +52,9 @@ def tile_picked_phpool_none_p_kernel(
         word_table = keep.tile([P, T], U32, name="word_table")
         nc.sync.dma_start(out=word_table[:].bitcast(I32), in_=x_words[0].rearrange("p n t -> p (n t)").bitcast(I32))
 
-        def pick_scales(first, last, tag):
+        def pick_scales(first, last, picked):
             plane = keep.tile([P, last - first], U8, name="x_plane_%d" % first, align_bytes=64)
             nc.vector.memset(plane[:].bitcast(I32), 0)
-            picked = keep.tile([P, last - first], U8, name="picked_%d" % first, tag=tag, align_bytes=64)
             nc.vector.tensor_copy(picked[:], byte_table[:].indirect(offsets[:, first // GROUP : last // GROUP]))
             for j in range(PACK):
                 nc.sync.dma_start(
@@ -62,14 +62,14 @@ def tile_picked_phpool_none_p_kernel(
                 )
             return plane
 
-        early_plane = pick_scales(0, EARLY, "picked")
+        early_picked = keep.tile([P, EARLY], U8, name="early_picked", tag="picked", align_bytes=64)
+        early_plane = pick_scales(0, EARLY, early_picked)
 
         grouped = keep.tile([P, PACK, P, PACK], BF16, name="grouped", align_bytes=64)
         dealt = grouped[:].rearrange("p t m j -> p m t j")
         source = w1_raw[:].rearrange("p (j m t) -> p m t j", j=PACK, t=PACK)
-        nc.scalar.copy(out=dealt[:, 0:SCALAR_GROUPS, :, 0], in_=source[:, 0:SCALAR_GROUPS, :, 0])
-        nc.scalar.copy(out=dealt[:, 0:SCALAR_GROUPS, :, 1:PACK], in_=source[:, 0:SCALAR_GROUPS, :, 1:PACK])
-        nc.vector.tensor_copy(out=dealt[:, SCALAR_GROUPS:P], in_=source[:, SCALAR_GROUPS:P])
+        nc.scalar.copy(out=dealt[:, VECTOR_GROUPS:P], in_=source[:, VECTOR_GROUPS:P])
+        nc.vector.tensor_copy(out=dealt[:, 0:VECTOR_GROUPS], in_=source[:, 0:VECTOR_GROUPS])
 
         w1_codes = keep.tile([P, H], U32, name="w1_codes", align_bytes=64)
         w1_plane = keep.tile([P, H], U8, name="w1_plane", align_bytes=64)
@@ -93,7 +93,8 @@ def tile_picked_phpool_none_p_kernel(
                 stop=True,
             )
 
-        late_plane = pick_scales(EARLY, S, "raw")
+        late_picked = reused.tile([P, S - EARLY], U8, name="late_picked", offset=PACK * S, align_bytes=64)
+        late_plane = pick_scales(EARLY, S, late_picked)
 
         w2_plane = keep.tile([P, N], U8, name="w2_plane", tag="table", align_bytes=64)
         for j in range(PACK):
@@ -110,7 +111,7 @@ def tile_picked_phpool_none_p_kernel(
 
         words = []
         for first in range(0, S, PIECE):
-            piece = keep.tile([P, PIECE], U32, name="words_%d" % first, tag="words_%d" % first, align_bytes=64)
+            piece = reused.tile([P, PIECE], U32, name="words_%d" % first, offset=PACK * first, align_bytes=64)
             nc.vector.tensor_copy(
                 piece[:], word_table[:].indirect(offsets[:, first // GROUP : (first + PIECE) // GROUP])
             )
@@ -151,36 +152,41 @@ def tile_picked_phpool_none_p_kernel(
             nc.vector.tensor_tensor(out=z[:], in0=y[(1, c)], in1=y[(0, c)], op=mybir.AluOpType.max)
             z_tiles[c] = z
 
-        def finish(c, slot, bank):
-            z_codes = keep.tile([P, CHUNK], U32, name="z_codes_%d" % c, tag=slot, align_bytes=64)
-            z_plane = keep.tile([P, CHUNK], U8, name="z_plane_%d" % c, align_bytes=64)
+        z_codes = keep.tile([P, V], U32, name="z_codes", align_bytes=64)
+        z_plane = keep.tile([P, V], U8, name="z_plane", align_bytes=64)
+
+        def quantise(c):
+            cols = slice(c * CHUNK, (c + 1) * CHUNK)
             nc.vector.quantize_mx(
-                out=z_codes[:].bitcast(FP8X4),
-                scales=z_plane[:],
+                out=z_codes[:, cols].bitcast(FP8X4),
+                scales=z_plane[:, cols],
                 in_=z_tiles[c][:].rearrange("p n t -> p (n t)"),
             )
-            acc = psum.tile([P, CHUNK], F32, name="acc_%d" % c, tag=bank)
+
+        def finish(first, count, bank, copy):
+            cols = slice(first * CHUNK, (first + count) * CHUNK)
+            acc = psum.tile([P, count * CHUNK], F32, name="acc_%d" % first, tag=bank)
             nc.tensor.matmul_mx(
                 out=acc[:],
                 lhsT=w2_codes[:].bitcast(FP4X4),
                 lhsT_scale=w2_plane[:],
-                rhs=z_codes[:].bitcast(FP8X4),
-                rhs_scale=z_plane[:],
+                rhs=z_codes[:, cols].bitcast(FP8X4),
+                rhs_scale=z_plane[:, cols],
                 start=True,
                 stop=True,
             )
-            result = keep.tile([P, CHUNK], F32, name="result_%d" % c)
-            if c == BOTH:
-                nc.vector.tensor_copy(out=result[:], in_=acc[:])
-            else:
-                nc.scalar.copy(out=result[:], in_=acc[:])
-            nc.sync.dma_start(out=out[:, c * CHUNK : (c + 1) * CHUNK], in_=result[:])
+            result = keep.tile([P, count * CHUNK], F32, name="result_%d" % first)
+            copy(out=result[:], in_=acc[:])
+            nc.sync.dma_start(out=out[:, cols], in_=result[:])
 
         larger(0)
         larger(1)
-        finish(0, "words_0", "y_1_%d" % BOTH)
+        quantise(0)
+        quantise(1)
+        finish(0, 2, "y_1_%d" % BOTH, nc.scalar.copy)
         larger(3)
-        finish(1, "words_%d" % (S - PIECE), "y_0_0")
         larger(BOTH)
-        finish(3, "words_%d" % PIECE, "y_0_1")
-        finish(BOTH, "words_%d" % (2 * PIECE), "y_0_2")
+        quantise(3)
+        finish(3, 1, "y_0_0", nc.scalar.copy)
+        quantise(BOTH)
+        finish(BOTH, 1, "y_0_1", nc.vector.tensor_copy)

@@ -22,9 +22,8 @@ GROUP = 16
 PIECE = 256
 CHUNK = 128
 CHUNKS = V // CHUNK
-LEAD_BANKS = 2
 W1_LEAD = 320
-VECTOR_GROUPS = 80
+VECTOR_GROUPS = 84
 EARLY = 768
 BOTH = 2
 
@@ -69,7 +68,10 @@ def tile_picked_phpool_none_p_kernel(
         dealt = grouped[:].rearrange("p t m j -> p m t j")
         source = w1_raw[:].rearrange("p (j m t) -> p m t j", j=PACK, t=PACK)
         nc.scalar.copy(out=dealt[:, VECTOR_GROUPS:P], in_=source[:, VECTOR_GROUPS:P])
-        nc.vector.tensor_copy(out=dealt[:, 0:VECTOR_GROUPS], in_=source[:, 0:VECTOR_GROUPS])
+        for first in range(0, PACK, 2):
+            nc.vector.tensor_copy(
+                out=dealt[:, 0:VECTOR_GROUPS, first : first + 2], in_=source[:, 0:VECTOR_GROUPS, first : first + 2]
+            )
 
         w1_codes = keep.tile([P, H], U32, name="w1_codes", align_bytes=64)
         w1_plane = keep.tile([P, H], U8, name="w1_plane", align_bytes=64)
@@ -109,17 +111,17 @@ def tile_picked_phpool_none_p_kernel(
                 return early_plane[:, entry : entry + CHUNK]
             return late_plane[:, entry - EARLY : entry - EARLY + CHUNK]
 
-        words = []
-        for first in range(0, S, PIECE):
+        words = {}
+        for first in (read * V + place for place in range(0, V, PIECE) for read in range(2)):
             piece = reused.tile([P, PIECE], U32, name="words_%d" % first, offset=PACK * first, align_bytes=64)
             nc.vector.tensor_copy(
                 piece[:], word_table[:].indirect(offsets[:, first // GROUP : (first + PIECE) // GROUP])
             )
-            words.append(piece)
+            words[first] = piece
 
         y = {}
-        for step in range(CHUNKS + LEAD_BANKS):
-            for read, c in ((0, step), (1, step - LEAD_BANKS)):
+        for step in range(CHUNKS + 1):
+            for read, c in ((0, step), (1, step - 1)):
                 if not 0 <= c < CHUNKS:
                     continue
                 bank = psum.tile([P, PACK, CHUNK], F32, name="y_%d_%d" % (read, c), tag="y_%d_%d" % (read, c))
@@ -131,7 +133,7 @@ def tile_picked_phpool_none_p_kernel(
                         out=bank[:, t, :],
                         lhsT=w1_codes[:, cols].bitcast(FP8X4),
                         lhsT_scale=w1_plane[:, cols],
-                        rhs=words[entry // PIECE][:, within : within + CHUNK].bitcast(FP8X4),
+                        rhs=words[entry - within][:, within : within + CHUNK].bitcast(FP8X4),
                         rhs_scale=x_scale(entry),
                         start=True,
                         stop=True,

@@ -23,11 +23,11 @@ PIECE = 256
 CHUNK = 128
 CHUNKS = V // CHUNK
 W1_LEAD = 320
-VECTOR_GROUPS = 84
+SCALAR_GROUPS = 52
 EARLY = 768
 BOTH = 2
 
-assert W1_LEAD <= PACK * VECTOR_GROUPS
+assert PACK * SCALAR_GROUPS <= W1_LEAD
 
 
 def tile_picked_phpool_none_p_kernel(
@@ -67,10 +67,11 @@ def tile_picked_phpool_none_p_kernel(
         grouped = keep.tile([P, PACK, P, PACK], BF16, name="grouped", align_bytes=64)
         dealt = grouped[:].rearrange("p t m j -> p m t j")
         source = w1_raw[:].rearrange("p (j m t) -> p m t j", j=PACK, t=PACK)
-        nc.scalar.copy(out=dealt[:, VECTOR_GROUPS:P], in_=source[:, VECTOR_GROUPS:P])
+        for rows in (slice(0, 1), slice(1, PACK)):
+            nc.scalar.copy(out=dealt[:, 0:SCALAR_GROUPS, :, rows], in_=source[:, 0:SCALAR_GROUPS, :, rows])
         for first in range(0, PACK, 2):
             nc.vector.tensor_copy(
-                out=dealt[:, 0:VECTOR_GROUPS, first : first + 2], in_=source[:, 0:VECTOR_GROUPS, first : first + 2]
+                out=dealt[:, SCALAR_GROUPS:P, first : first + 2], in_=source[:, SCALAR_GROUPS:P, first : first + 2]
             )
 
         w1_codes = keep.tile([P, H], U32, name="w1_codes", align_bytes=64)
@@ -106,10 +107,10 @@ def tile_picked_phpool_none_p_kernel(
         w2_codes = keep.tile([P, 2 * N], U8, name="w2_codes", tag="picked", align_bytes=64)
         nc.sync.dma_start(out=w2_codes[:].bitcast(I32), in_=w2_words[0].bitcast(I32))
 
-        def x_scale(entry):
+        def x_scale(entry, width):
             if entry < EARLY:
-                return early_plane[:, entry : entry + CHUNK]
-            return late_plane[:, entry - EARLY : entry - EARLY + CHUNK]
+                return early_plane[:, entry : entry + width]
+            return late_plane[:, entry - EARLY : entry - EARLY + width]
 
         words = {}
         for first in (read * V + place for place in range(0, V, PIECE) for read in range(2)):
@@ -119,39 +120,50 @@ def tile_picked_phpool_none_p_kernel(
             )
             words[first] = piece
 
+        def first_product(bank_out, t, entry, width):
+            cols = slice(t * P, (t + 1) * P)
+            within = entry % PIECE
+            nc.tensor.matmul_mx(
+                out=bank_out,
+                lhsT=w1_codes[:, cols].bitcast(FP8X4),
+                lhsT_scale=w1_plane[:, cols],
+                rhs=words[entry - within][:, within : within + width].bitcast(FP8X4),
+                rhs_scale=x_scale(entry, width),
+                start=True,
+                stop=True,
+            )
+
         y = {}
+        wide = keep.tile([P, 2, PIECE, 2], BF16, name="wide")
         for step in range(CHUNKS + 1):
             for read, c in ((0, step), (1, step - 1)):
                 if not 0 <= c < CHUNKS:
                     continue
-                bank = psum.tile([P, PACK, CHUNK], F32, name="y_%d_%d" % (read, c), tag="y_%d_%d" % (read, c))
-                entry = read * V + c * CHUNK
-                within = entry % PIECE
+                name = "y_%d_%d" % (read, c)
+                if read == 0 and c >= 2:
+                    pair = c - 2
+                    bank = psum.tile([P, 2, PIECE], F32, name=name, tag=name)
+                    for t in range(2):
+                        first_product(bank[:, t, :], 2 * pair + t, PIECE, PIECE)
+                    nc.scalar.copy(out=wide[:, pair], in_=bank[:].rearrange("p t n -> p n t"))
+                    y[(read, c)] = wide[:, :, pair * CHUNK : (pair + 1) * CHUNK].rearrange("p u n t -> p n u t")
+                    continue
+                bank = psum.tile([P, PACK, CHUNK], F32, name=name, tag=name)
                 for t in range(PACK):
-                    cols = slice(t * P, (t + 1) * P)
-                    nc.tensor.matmul_mx(
-                        out=bank[:, t, :],
-                        lhsT=w1_codes[:, cols].bitcast(FP8X4),
-                        lhsT_scale=w1_plane[:, cols],
-                        rhs=words[entry - within][:, within : within + CHUNK].bitcast(FP8X4),
-                        rhs_scale=x_scale(entry),
-                        start=True,
-                        stop=True,
-                    )
+                    first_product(bank[:, t, :], t, read * V + c * CHUNK, CHUNK)
                 interleaved = bank[:].rearrange("p t n -> p n t")
                 both = c == BOTH
                 if read == 0 or both:
                     copied = keep.tile([P, CHUNK, PACK], BF16 if both else F32, name="copied_%d_%d" % (read, c))
                     nc.scalar.copy(out=copied[:], in_=interleaved)
-                    y[(read, c)] = copied[:]
-                else:
-                    y[(read, c)] = interleaved
+                    interleaved = copied[:]
+                y[(read, c)] = interleaved.rearrange("p n (u t) -> p n u t", u=2)
 
         z_tiles = {}
 
         def larger(c):
             z = keep.tile([P, CHUNK, PACK], BF16, name="z_%d" % c, align_bytes=64)
-            nc.vector.tensor_tensor(out=z[:], in0=y[(1, c)], in1=y[(0, c)], op=mybir.AluOpType.max)
+            nc.vector.tensor_tensor(out=z[:].rearrange("p n (u t) -> p n u t", u=2), in0=y[(1, c)], in1=y[(0, c)], op=mybir.AluOpType.max)
             z_tiles[c] = z
 
         z_codes = keep.tile([P, V], U32, name="z_codes", align_bytes=64)

@@ -40,15 +40,15 @@ def tile_picked_phpool_none_p_kernel(
         psum = ctx.enter_context(tc.psum_pool(name="psum", bufs=1))
 
         offsets = keep.tile([P, S // GROUP], U16, name="offsets")
-        byte_table = keep.tile([P, T], U8, name="byte_table", tag="table", align_bytes=64)
+        byte_table = keep.tile([P, T], U8, name="byte_table", tag="table", align_bytes=256)
         nc.vector.memset(byte_table[:].bitcast(I32), 0)
         w1_rows = w1.rearrange("(p j) c -> p (j c)", j=PACK)
-        w1_raw = reused.tile([P, PACK * H], F32, name="w1_raw", offset=0, align_bytes=64)
+        w1_raw = reused.tile([P, PACK * H], F32, name="w1_raw", offset=0, align_bytes=256)
         nc.sync.dma_start(out=w1_raw[:, 0:W1_LEAD], in_=w1_rows[:, 0:W1_LEAD])
         nc.sync.dma_start(offsets[:], offs)
         nc.sync.dma_start(out=byte_table[0:P:BLOCK, :].bitcast(I32), in_=x_scales[0].bitcast(I32))
         nc.sync.dma_start(out=w1_raw[:, W1_LEAD : PACK * H], in_=w1_rows[:, W1_LEAD : PACK * H])
-        word_table = keep.tile([P, T], U32, name="word_table")
+        word_table = keep.tile([P, T], U32, name="word_table", align_bytes=256)
         nc.sync.dma_start(out=word_table[:].bitcast(I32), in_=x_words[0].rearrange("p n t -> p (n t)").bitcast(I32))
 
         def pick_scales(first, last, picked):
@@ -99,7 +99,7 @@ def tile_picked_phpool_none_p_kernel(
         late_picked = reused.tile([P, S - EARLY], U8, name="late_picked", offset=PACK * S, align_bytes=64)
         late_plane = pick_scales(EARLY, S, late_picked)
 
-        w2_plane = keep.tile([P, N], U8, name="w2_plane", tag="table", align_bytes=64)
+        w2_plane = keep.tile([P, N], U8, name="w2_plane", tag="table", align_bytes=256)
         for j in range(PACK):
             nc.sync.dma_start(
                 out=w2_plane[j:P:QUAD, :].bitcast(I32), in_=w2_scales[0, j : H // QUAD : PACK, :].bitcast(I32)
@@ -189,7 +189,7 @@ def tile_picked_phpool_none_p_kernel(
                 start=True,
                 stop=True,
             )
-            result = keep.tile([P, count * CHUNK], F32, name="result_%d" % first)
+            result = keep.tile([P, count * CHUNK], F32, name="result_%d" % first, align_bytes=256)
             copy(out=result[:], in_=acc[:])
             nc.sync.dma_start(out=out[:, cols], in_=result[:])
 

@@ -22,7 +22,7 @@ GROUP = 16
 PIECE = 256
 CHUNK = 128
 CHUNKS = V // CHUNK
-W1_LEAD = 320
+W1_LEAD = 256
 SCALAR_GROUPS = 52
 EARLY = 768
 BOTH = 2

@@ -23,6 +23,7 @@ PIECE = 256
 CHUNK = 128
 CHUNKS = V // CHUNK
 W1_LEAD = 256
+W1_TAIL = 256
 SCALAR_GROUPS = 52
 EARLY = 768
 BOTH = 2
@@ -47,7 +48,9 @@ def tile_picked_phpool_none_p_kernel(
         nc.sync.dma_start(out=w1_raw[:, 0:W1_LEAD], in_=w1_rows[:, 0:W1_LEAD])
         nc.sync.dma_start(offsets[:], offs)
         nc.sync.dma_start(out=byte_table[0:P:BLOCK, :].bitcast(I32), in_=x_scales[0].bitcast(I32))
-        nc.sync.dma_start(out=w1_raw[:, W1_LEAD : PACK * H], in_=w1_rows[:, W1_LEAD : PACK * H])
+        tail = PACK * H - W1_TAIL
+        nc.sync.dma_start(out=w1_raw[:, W1_LEAD:tail], in_=w1_rows[:, W1_LEAD:tail])
+        nc.sync.dma_start(out=w1_raw[:, tail : PACK * H], in_=w1_rows[:, tail : PACK * H])
         word_table = keep.tile([P, T], U32, name="word_table", align_bytes=256)
         nc.sync.dma_start(out=word_table[:].bitcast(I32), in_=x_words[0].rearrange("p n t -> p (n t)").bitcast(I32))
 
@@ -69,10 +72,10 @@ def tile_picked_phpool_none_p_kernel(
         source = w1_raw[:].rearrange("p (j m t) -> p m t j", j=PACK, t=PACK)
         for rows in (slice(0, 1), slice(1, PACK)):
             nc.scalar.copy(out=dealt[:, 0:SCALAR_GROUPS, :, rows], in_=source[:, 0:SCALAR_GROUPS, :, rows])
+        whole = (H - W1_TAIL) // PACK
+        nc.vector.tensor_copy(out=dealt[:, SCALAR_GROUPS:whole], in_=source[:, SCALAR_GROUPS:whole])
         for first in range(0, PACK, 2):
-            nc.vector.tensor_copy(
-                out=dealt[:, SCALAR_GROUPS:P, first : first + 2], in_=source[:, SCALAR_GROUPS:P, first : first + 2]
-            )
+            nc.vector.tensor_copy(out=dealt[:, whole:P, first : first + 2], in_=source[:, whole:P, first : first + 2])
 
         w1_codes = keep.tile([P, H], U32, name="w1_codes", align_bytes=64)
         w1_plane = keep.tile([P, H], U8, name="w1_plane", align_bytes=64)
@@ -197,7 +200,8 @@ def tile_picked_phpool_none_p_kernel(
         larger(1)
         quantise(0)
         quantise(1)
-        finish(0, 2, "y_1_%d" % BOTH, nc.scalar.copy)
+        finish(0, 1, "y_0_%d" % (CHUNKS - 1), nc.scalar.copy)
+        finish(1, 1, "y_1_%d" % BOTH, nc.scalar.copy)
         larger(3)
         larger(BOTH)
         quantise(3)

@@ -24,7 +24,8 @@ CHUNK = 128
 CHUNKS = V // CHUNK
 W1_LEAD = 256
 W1_TAIL = 256
-SCALAR_GROUPS = 52
+SCALAR_TAIL = 14
+SCALAR_GROUPS = 40
 EARLY = 768
 BOTH = 2
 
@@ -74,8 +75,12 @@ def tile_picked_phpool_none_p_kernel(
             nc.scalar.copy(out=dealt[:, 0:SCALAR_GROUPS, :, rows], in_=source[:, 0:SCALAR_GROUPS, :, rows])
         whole = (H - W1_TAIL) // PACK
         nc.vector.tensor_copy(out=dealt[:, SCALAR_GROUPS:whole], in_=source[:, SCALAR_GROUPS:whole])
+        split = P - SCALAR_TAIL
+        nc.scalar.copy(out=dealt[:, split:P], in_=source[:, split:P])
         for first in range(0, PACK, 2):
-            nc.vector.tensor_copy(out=dealt[:, whole:P, first : first + 2], in_=source[:, whole:P, first : first + 2])
+            nc.vector.tensor_copy(
+                out=dealt[:, whole:split, first : first + 2], in_=source[:, whole:split, first : first + 2]
+            )
 
         w1_codes = keep.tile([P, H], U32, name="w1_codes", align_bytes=64)
         w1_plane = keep.tile([P, H], U8, name="w1_plane", align_bytes=64)

@@ -28,6 +28,7 @@ SCALAR_TAIL = 14
 SCALAR_GROUPS = 40
 EARLY = 768
 BOTH = 2
+THIN = 32
 
 assert PACK * SCALAR_GROUPS <= W1_LEAD
 
@@ -93,11 +94,11 @@ def tile_picked_phpool_none_p_kernel(
             )
 
         warm = psum.tile([P, H], F32, name="warm", tag="y_1_%d" % (CHUNKS - 1))
-        for rows, columns in ((128, 256), (64, 512), (64, 512),):
+        for columns in (CHUNK, CHUNK, H, H):
             nc.tensor.matmul_mx(
-                out=warm[0:rows, 0:columns],
-                lhsT=w1_codes[:, 0:rows].bitcast(FP8X4),
-                lhsT_scale=w1_plane[:, 0:rows],
+                out=warm[0:THIN, 0:columns],
+                lhsT=w1_codes[:, 0:THIN].bitcast(FP8X4),
+                lhsT_scale=w1_plane[:, 0:THIN],
                 rhs=w1_codes[:, 0:columns].bitcast(FP8X4),
                 rhs_scale=w1_plane[:, 0:columns],
                 start=True,

@@ -93,7 +93,7 @@ def tile_picked_phpool_none_p_kernel(
                 in_=grouped[:, first : first + 2].rearrange("p t m j -> p (t m j)"),
             )
 
-        warm = psum.tile([P, H], F32, name="warm", tag="y_1_%d" % (CHUNKS - 1))
+        warm = psum.tile([P, H], F32, name="warm", tag="y_1_%d" % BOTH)
         for columns in (CHUNK, CHUNK, H, H):
             nc.tensor.matmul_mx(
                 out=warm[0:THIN, 0:columns],
@@ -149,6 +149,15 @@ def tile_picked_phpool_none_p_kernel(
                 if not 0 <= c < CHUNKS:
                     continue
                 name = "y_%d_%d" % (read, c)
+                if read == 0 and c == 0:
+                    halves = keep.tile([P, 2, CHUNK, 2], F32, name="halves")
+                    for pair, tag in enumerate(("y_1_%d" % (CHUNKS - 1), name)):
+                        bank = psum.tile([P, 2, CHUNK], F32, name="first_%d" % pair, tag=tag)
+                        for t in range(2):
+                            first_product(bank[:, t, :], 2 * pair + t, 0, CHUNK)
+                        nc.scalar.copy(out=halves[:, pair], in_=bank[:].rearrange("p t n -> p n t"))
+                    y[(read, c)] = halves[:].rearrange("p u n t -> p n u t")
+                    continue
                 if read == 0 and c >= 2:
                     pair = c - 2
                     bank = psum.tile([P, 2, PIECE], F32, name=name, tag=name)
@@ -205,10 +214,10 @@ def tile_picked_phpool_none_p_kernel(
         larger(0)
         larger(1)
         quantise(0)
-        quantise(1)
         finish(0, 1, "y_0_%d" % (CHUNKS - 1), nc.scalar.copy)
-        finish(1, 1, "y_1_%d" % BOTH, nc.scalar.copy)
         larger(3)
+        quantise(1)
+        finish(1, 1, "y_1_%d" % BOTH, nc.scalar.copy)
         larger(BOTH)
         quantise(3)
         finish(3, 1, "y_0_0", nc.scalar.copy)

@@ -142,46 +142,45 @@ def tile_picked_phpool_none_p_kernel(
                 stop=True,
             )
 
+        def by_tile(ap):
+            return ap.rearrange("p t (a b) -> p a t b", b=2)
+
+        def by_place(ap):
+            return ap.rearrange("p (a b) t -> p a t b", b=2)
+
         y = {}
-        wide = keep.tile([P, 2, PIECE, 2], BF16, name="wide")
-        for step in range(CHUNKS + 1):
-            for read, c in ((0, step), (1, step - 1)):
-                if not 0 <= c < CHUNKS:
-                    continue
-                name = "y_%d_%d" % (read, c)
-                if read == 0 and c == 0:
-                    halves = keep.tile([P, 2, CHUNK, 2], F32, name="halves")
-                    for pair, tag in enumerate(("y_1_%d" % (CHUNKS - 1), name)):
-                        bank = psum.tile([P, 2, CHUNK], F32, name="first_%d" % pair, tag=tag)
-                        for t in range(2):
-                            first_product(bank[:, t, :], 2 * pair + t, 0, CHUNK)
-                        nc.scalar.copy(out=halves[:, pair], in_=bank[:].rearrange("p t n -> p n t"))
-                    y[(read, c)] = halves[:].rearrange("p u n t -> p n u t")
-                    continue
-                if read == 0 and c >= 2:
-                    pair = c - 2
-                    bank = psum.tile([P, 2, PIECE], F32, name=name, tag=name)
+        for read, c in ((0, 0), (0, 1), (1, 0), (0, 3), (1, 1), (0, 2), (1, 2), (1, 3)):
+            name = "y_%d_%d" % (read, c)
+            if read == 0 and c == 0:
+                halves = keep.tile([P, PACK, CHUNK], F32, name="halves")
+                for pair, tag in enumerate(("y_1_%d" % (CHUNKS - 1), name)):
+                    bank = psum.tile([P, 2, CHUNK], F32, name="first_%d" % pair, tag=tag)
                     for t in range(2):
-                        first_product(bank[:, t, :], 2 * pair + t, PIECE, PIECE)
-                    nc.scalar.copy(out=wide[:, pair], in_=bank[:].rearrange("p t n -> p n t"))
-                    y[(read, c)] = wide[:, :, pair * CHUNK : (pair + 1) * CHUNK].rearrange("p u n t -> p n u t")
-                    continue
-                bank = psum.tile([P, PACK, CHUNK], F32, name=name, tag=name)
-                for t in range(PACK):
-                    first_product(bank[:, t, :], t, read * V + c * CHUNK, CHUNK)
-                interleaved = bank[:].rearrange("p t n -> p n t")
-                both = c == BOTH
-                if read == 0 or both:
-                    copied = keep.tile([P, CHUNK, PACK], BF16 if both else F32, name="copied_%d_%d" % (read, c))
-                    nc.scalar.copy(out=copied[:], in_=interleaved)
-                    interleaved = copied[:]
-                y[(read, c)] = interleaved.rearrange("p n (u t) -> p n u t", u=2)
+                        first_product(bank[:, t, :], 2 * pair + t, 0, CHUNK)
+                    nc.scalar.copy(out=halves[:, 2 * pair : 2 * pair + 2], in_=bank[:])
+                y[(read, c)] = by_tile(halves[:])
+                continue
+            bank = psum.tile([P, PACK, CHUNK], F32, name=name, tag=name)
+            for t in range(PACK):
+                first_product(bank[:, t, :], t, read * V + c * CHUNK, CHUNK)
+            if c == BOTH:
+                copied = keep.tile([P, CHUNK, PACK], BF16, name="copied_%d_%d" % (read, c))
+                nc.scalar.copy(out=by_place(copied[:]), in_=by_tile(bank[:]))
+                y[(read, c)] = copied[:]
+            elif read == 0:
+                copied = keep.tile([P, PACK, CHUNK], F32, name="copied_%d_%d" % (read, c))
+                nc.scalar.copy(out=copied[:], in_=bank[:])
+                y[(read, c)] = by_tile(copied[:])
+            else:
+                y[(read, c)] = by_tile(bank[:])
 
         z_tiles = {}
 
         def larger(c):
             z = keep.tile([P, CHUNK, PACK], BF16, name="z_%d" % c, align_bytes=64)
-            nc.vector.tensor_tensor(out=z[:].rearrange("p n (u t) -> p n u t", u=2), in0=y[(1, c)], in1=y[(0, c)], op=mybir.AluOpType.max)
+            nc.vector.tensor_tensor(
+                out=z[:] if c == BOTH else by_place(z[:]), in0=y[(1, c)], in1=y[(0, c)], op=mybir.AluOpType.max
+            )
             z_tiles[c] = z
 
         z_codes = keep.tile([P, V], U32, name="z_codes", align_bytes=64)
@@ -214,7 +213,7 @@ def tile_picked_phpool_none_p_kernel(
         larger(0)
         larger(1)
         quantise(0)
-        finish(0, 1, "y_0_%d" % (CHUNKS - 1), nc.scalar.copy)
+        finish(0, 1, "y_0_%d" % BOTH, nc.scalar.copy)
         larger(3)
         quantise(1)
         finish(1, 1, "y_1_%d" % BOTH, nc.scalar.copy)

@@ -24,8 +24,9 @@ CHUNK = 128
 CHUNKS = V // CHUNK
 W1_LEAD = 256
 W1_TAIL = 256
-SCALAR_TAIL = 14
-SCALAR_GROUPS = 40
+HALF = P // 2
+SCALAR_TAIL = 32
+SCALAR_GROUPS = 32
 EARLY = 768
 BOTH = 2
 THIN = 32
@@ -69,38 +70,54 @@ def tile_picked_phpool_none_p_kernel(
         early_picked = keep.tile([P, EARLY], U8, name="early_picked", tag="picked", align_bytes=64)
         early_plane = pick_scales(0, EARLY, early_picked)
 
-        grouped = keep.tile([P, PACK, P, PACK], BF16, name="grouped", align_bytes=64)
-        dealt = grouped[:].rearrange("p t m j -> p m t j")
         source = w1_raw[:].rearrange("p (j m t) -> p m t j", j=PACK, t=PACK)
+        lower = keep.tile([P, PACK, HALF, PACK], BF16, name="lower", align_bytes=64)
+        upper = keep.tile([P, PACK, HALF, PACK], BF16, name="upper", align_bytes=64)
+        dealt = lower[:].rearrange("p t m j -> p m t j")
         for rows in (slice(0, 1), slice(1, PACK)):
             nc.scalar.copy(out=dealt[:, 0:SCALAR_GROUPS, :, rows], in_=source[:, 0:SCALAR_GROUPS, :, rows])
-        whole = (H - W1_TAIL) // PACK
-        nc.vector.tensor_copy(out=dealt[:, SCALAR_GROUPS:whole], in_=source[:, SCALAR_GROUPS:whole])
-        split = P - SCALAR_TAIL
-        nc.scalar.copy(out=dealt[:, split:P], in_=source[:, split:P])
-        for first in range(0, PACK, 2):
-            nc.vector.tensor_copy(
-                out=dealt[:, whole:split, first : first + 2], in_=source[:, whole:split, first : first + 2]
-            )
+        nc.vector.tensor_copy(out=dealt[:, SCALAR_GROUPS:HALF], in_=source[:, SCALAR_GROUPS:HALF])
+
+        staged_codes = keep.tile([P, PACK * HALF], U32, name="staged_codes", align_bytes=64)
+        staged_plane = keep.tile([P, PACK * HALF], U8, name="staged_plane", align_bytes=64)
+        nc.vector.memset(staged_plane[:].bitcast(I32), 0)
+        nc.vector.quantize_mx(
+            out=staged_codes[:].bitcast(FP8X4),
+            scales=staged_plane[:],
+            in_=lower[:].rearrange("p t m j -> p (t m j)"),
+        )
+
+        dealt = upper[:].rearrange("p t m j -> p m t j")
+        split = HALF - SCALAR_TAIL
+        nc.scalar.copy(out=dealt[:, split:HALF], in_=source[:, HALF + split : P])
+        nc.vector.tensor_copy(out=dealt[:, 0:split], in_=source[:, HALF : HALF + split])
 
         w1_codes = keep.tile([P, H], U32, name="w1_codes", align_bytes=64)
         w1_plane = keep.tile([P, H], U8, name="w1_plane", align_bytes=64)
-        for first in range(0, PACK, 2):
-            cols = slice(first * P, (first + 2) * P)
+        for t in range(PACK):
+            cols = slice(t * P + HALF, (t + 1) * P)
             nc.vector.quantize_mx(
                 out=w1_codes[:, cols].bitcast(FP8X4),
                 scales=w1_plane[:, cols],
-                in_=grouped[:, first : first + 2].rearrange("p t m j -> p (t m j)"),
+                in_=upper[:, t].rearrange("p m j -> p (m j)"),
             )
+        nc.scalar.copy(
+            out=w1_codes[:].rearrange("p (t m) -> p t m", t=PACK)[:, :, 0:HALF],
+            in_=staged_codes[:].rearrange("p (t m) -> p t m", t=PACK),
+        )
+        nc.scalar.copy(
+            out=w1_plane[:].rearrange("p (t m) -> p t m", t=PACK)[:, :, 0:HALF].bitcast(U32),
+            in_=staged_plane[:].rearrange("p (t m) -> p t m", t=PACK).bitcast(U32),
+        )
 
         warm = psum.tile([P, H], F32, name="warm", tag="y_1_%d" % BOTH)
-        for columns in (CHUNK, CHUNK, H, H):
+        for codes, plane, columns in ((staged_codes, staged_plane, CHUNK),) * 5 + ((w1_codes, w1_plane, H),):
             nc.tensor.matmul_mx(
                 out=warm[0:THIN, 0:columns],
-                lhsT=w1_codes[:, 0:THIN].bitcast(FP8X4),
-                lhsT_scale=w1_plane[:, 0:THIN],
-                rhs=w1_codes[:, 0:columns].bitcast(FP8X4),
-                rhs_scale=w1_plane[:, 0:columns],
+                lhsT=codes[:, 0:THIN].bitcast(FP8X4),
+                lhsT_scale=plane[:, 0:THIN],
+                rhs=codes[:, 0:columns].bitcast(FP8X4),
+                rhs_scale=plane[:, 0:columns],
                 start=True,
                 stop=True,
             )

from contextlib import ExitStack

import concourse.mybir as mybir

K, T, S, H, N, V = 512, 2048, 1024, 512, 128, 512
FLOPS = 2 * K * H * S + 2 * H * N * V

F32 = mybir.dt.float32
BF16 = mybir.dt.bfloat16
I32 = mybir.dt.int32
U32 = mybir.dt.uint32
U16 = mybir.dt.uint16
U8 = mybir.dt.uint8
FP8X4 = mybir.dt.float8_e4m3fn_x4
FP4X4 = mybir.dt.float4_e2m1fn_x4

P = 128
PACK = 4
QUAD = 32
BLOCK = 8
GROUP = 16
PIECE = 256
CHUNK = 128
CHUNKS = V // CHUNK
W1_LEAD = 256
W1_TAIL = 256
HALF = P // 2
SCALAR_TAIL = 32
SCALAR_GROUPS = 32
EARLY = 768
BOTH = 2
THIN = 32

assert PACK * SCALAR_GROUPS <= W1_LEAD


def tile_picked_phpool_none_p_kernel(
    tc, x_words, x_scales, w1, w2_words, w2_scales, offs, out
):
    nc = tc.nc
    with ExitStack() as ctx:
        keep = ctx.enter_context(tc.tile_pool(name="keep", bufs=1))
        reused = ctx.enter_context(tc.tile_pool(name="reused", bufs=1))
        psum = ctx.enter_context(tc.psum_pool(name="psum", bufs=1))

        offsets = keep.tile([P, S // GROUP], U16, name="offsets")
        byte_table = keep.tile([P, T], U8, name="byte_table", tag="table", align_bytes=256)
        nc.vector.memset(byte_table[:].bitcast(I32), 0)
        w1_rows = w1.rearrange("(p j) c -> p (j c)", j=PACK)
        w1_raw = reused.tile([P, PACK * H], F32, name="w1_raw", offset=0, align_bytes=256)
        nc.sync.dma_start(out=w1_raw[:, 0:W1_LEAD], in_=w1_rows[:, 0:W1_LEAD])
        nc.sync.dma_start(offsets[:], offs)
        nc.sync.dma_start(out=byte_table[0:P:BLOCK, :].bitcast(I32), in_=x_scales[0].bitcast(I32))
        tail = PACK * H - W1_TAIL
        nc.sync.dma_start(out=w1_raw[:, W1_LEAD:tail], in_=w1_rows[:, W1_LEAD:tail])
        nc.sync.dma_start(out=w1_raw[:, tail : PACK * H], in_=w1_rows[:, tail : PACK * H])
        word_table = keep.tile([P, T], U32, name="word_table", align_bytes=256)
        nc.sync.dma_start(out=word_table[:].bitcast(I32), in_=x_words[0].rearrange("p n t -> p (n t)").bitcast(I32))

        def pick_scales(first, last, picked):
            plane = keep.tile([P, last - first], U8, name="x_plane_%d" % first, align_bytes=64)
            nc.vector.memset(plane[:].bitcast(I32), 0)
            nc.vector.tensor_copy(picked[:], byte_table[:].indirect(offsets[:, first // GROUP : last // GROUP]))
            for j in range(PACK):
                nc.sync.dma_start(
                    out=plane[j:P:QUAD, :].bitcast(I32), in_=picked[BLOCK * j : P : QUAD, :].bitcast(I32)
                )
            return plane

        early_picked = keep.tile([P, EARLY], U8, name="early_picked", tag="picked", align_bytes=64)
        early_plane = pick_scales(0, EARLY, early_picked)

        source = w1_raw[:].rearrange("p (j m t) -> p m t j", j=PACK, t=PACK)
        lower = keep.tile([P, PACK, HALF, PACK], BF16, name="lower", align_bytes=64)
        upper = keep.tile([P, PACK, HALF, PACK], BF16, name="upper", align_bytes=64)
        dealt = lower[:].rearrange("p t m j -> p m t j")
        for rows in (slice(0, 1), slice(1, PACK)):
            nc.scalar.copy(out=dealt[:, 0:SCALAR_GROUPS, :, rows], in_=source[:, 0:SCALAR_GROUPS, :, rows])
        nc.vector.tensor_copy(out=dealt[:, SCALAR_GROUPS:HALF], in_=source[:, SCALAR_GROUPS:HALF])

        staged_codes = keep.tile([P, PACK * HALF], U32, name="staged_codes", align_bytes=64)
        staged_plane = keep.tile([P, PACK * HALF], U8, name="staged_plane", align_bytes=64)
        nc.vector.memset(staged_plane[:].bitcast(I32), 0)
        nc.vector.quantize_mx(
            out=staged_codes[:].bitcast(FP8X4),
            scales=staged_plane[:],
            in_=lower[:].rearrange("p t m j -> p (t m j)"),
        )

        dealt = upper[:].rearrange("p t m j -> p m t j")
        split = HALF - SCALAR_TAIL
        nc.scalar.copy(out=dealt[:, split:HALF], in_=source[:, HALF + split : P])
        nc.vector.tensor_copy(out=dealt[:, 0:split], in_=source[:, HALF : HALF + split])

        w1_codes = keep.tile([P, H], U32, name="w1_codes", align_bytes=64)
        w1_plane = keep.tile([P, H], U8, name="w1_plane", align_bytes=64)
        for t in range(PACK):
            cols = slice(t * P + HALF, (t + 1) * P)
            nc.vector.quantize_mx(
                out=w1_codes[:, cols].bitcast(FP8X4),
                scales=w1_plane[:, cols],
                in_=upper[:, t].rearrange("p m j -> p (m j)"),
            )
        nc.scalar.copy(
            out=w1_codes[:].rearrange("p (t m) -> p t m", t=PACK)[:, :, 0:HALF],
            in_=staged_codes[:].rearrange("p (t m) -> p t m", t=PACK),
        )
        nc.scalar.copy(
            out=w1_plane[:].rearrange("p (t m) -> p t m", t=PACK)[:, :, 0:HALF].bitcast(U32),
            in_=staged_plane[:].rearrange("p (t m) -> p t m", t=PACK).bitcast(U32),
        )

        warm = psum.tile([P, H], F32, name="warm", tag="y_1_%d" % BOTH)
        for codes, plane, columns in ((staged_codes, staged_plane, CHUNK),) * 5 + ((w1_codes, w1_plane, H),):
            nc.tensor.matmul_mx(
                out=warm[0:THIN, 0:columns],
                lhsT=codes[:, 0:THIN].bitcast(FP8X4),
                lhsT_scale=plane[:, 0:THIN],
                rhs=codes[:, 0:columns].bitcast(FP8X4),
                rhs_scale=plane[:, 0:columns],
                start=True,
                stop=True,
            )

        late_picked = reused.tile([P, S - EARLY], U8, name="late_picked", offset=PACK * S, align_bytes=64)
        late_plane = pick_scales(EARLY, S, late_picked)

        w2_plane = keep.tile([P, N], U8, name="w2_plane", tag="table", align_bytes=256)
        for j in range(PACK):
            nc.sync.dma_start(
                out=w2_plane[j:P:QUAD, :].bitcast(I32), in_=w2_scales[0, j : H // QUAD : PACK, :].bitcast(I32)
            )
        w2_codes = keep.tile([P, 2 * N], U8, name="w2_codes", tag="picked", align_bytes=64)
        nc.sync.dma_start(out=w2_codes[:].bitcast(I32), in_=w2_words[0].bitcast(I32))

        def x_scale(entry, width):
            if entry < EARLY:
                return early_plane[:, entry : entry + width]
            return late_plane[:, entry - EARLY : entry - EARLY + width]

        words = {}
        for first in (read * V + place for place in range(0, V, PIECE) for read in range(2)):
            piece = reused.tile([P, PIECE], U32, name="words_%d" % first, offset=PACK * first, align_bytes=64)
            nc.vector.tensor_copy(
                piece[:], word_table[:].indirect(offsets[:, first // GROUP : (first + PIECE) // GROUP])
            )
            words[first] = piece

        def first_product(bank_out, t, entry, width):
            cols = slice(t * P, (t + 1) * P)
            within = entry % PIECE
            nc.tensor.matmul_mx(
                out=bank_out,
                lhsT=w1_codes[:, cols].bitcast(FP8X4),
                lhsT_scale=w1_plane[:, cols],
                rhs=words[entry - within][:, within : within + width].bitcast(FP8X4),
                rhs_scale=x_scale(entry, width),
                start=True,
                stop=True,
            )

        def by_tile(ap):
            return ap.rearrange("p t (a b) -> p a t b", b=2)

        def by_place(ap):
            return ap.rearrange("p (a b) t -> p a t b", b=2)

        y = {}
        for read, c in ((0, 0), (0, 1), (1, 0), (0, 3), (1, 1), (0, 2), (1, 2), (1, 3)):
            name = "y_%d_%d" % (read, c)
            if read == 0 and c == 0:
                halves = keep.tile([P, PACK, CHUNK], F32, name="halves")
                for pair, tag in enumerate(("y_1_%d" % (CHUNKS - 1), name)):
                    bank = psum.tile([P, 2, CHUNK], F32, name="first_%d" % pair, tag=tag)
                    for t in range(2):
                        first_product(bank[:, t, :], 2 * pair + t, 0, CHUNK)
                    nc.scalar.copy(out=halves[:, 2 * pair : 2 * pair + 2], in_=bank[:])
                y[(read, c)] = by_tile(halves[:])
                continue
            bank = psum.tile([P, PACK, CHUNK], F32, name=name, tag=name)
            for t in range(PACK):
                first_product(bank[:, t, :], t, read * V + c * CHUNK, CHUNK)
            if c == BOTH:
                copied = keep.tile([P, CHUNK, PACK], BF16, name="copied_%d_%d" % (read, c))
                nc.scalar.copy(out=by_place(copied[:]), in_=by_tile(bank[:]))
                y[(read, c)] = copied[:]
            elif read == 0:
                copied = keep.tile([P, PACK, CHUNK], F32, name="copied_%d_%d" % (read, c))
                nc.scalar.copy(out=copied[:], in_=bank[:])
                y[(read, c)] = by_tile(copied[:])
            else:
                y[(read, c)] = by_tile(bank[:])

        z_tiles = {}

        def larger(c):
            z = keep.tile([P, CHUNK, PACK], BF16, name="z_%d" % c, align_bytes=64)
            nc.vector.tensor_tensor(
                out=z[:] if c == BOTH else by_place(z[:]), in0=y[(1, c)], in1=y[(0, c)], op=mybir.AluOpType.max
            )
            z_tiles[c] = z

        z_codes = keep.tile([P, V], U32, name="z_codes", align_bytes=64)
        z_plane = keep.tile([P, V], U8, name="z_plane", align_bytes=64)

        def quantise(c):
            cols = slice(c * CHUNK, (c + 1) * CHUNK)
            nc.vector.quantize_mx(
                out=z_codes[:, cols].bitcast(FP8X4),
                scales=z_plane[:, cols],
                in_=z_tiles[c][:].rearrange("p n t -> p (n t)"),
            )

        def finish(first, count, bank, copy):
            cols = slice(first * CHUNK, (first + count) * CHUNK)
            acc = psum.tile([P, count * CHUNK], F32, name="acc_%d" % first, tag=bank)
            nc.tensor.matmul_mx(
                out=acc[:],
                lhsT=w2_codes[:].bitcast(FP4X4),
                lhsT_scale=w2_plane[:],
                rhs=z_codes[:, cols].bitcast(FP8X4),
                rhs_scale=z_plane[:, cols],
                start=True,
                stop=True,
            )
            result = keep.tile([P, count * CHUNK], F32, name="result_%d" % first, align_bytes=256)
            copy(out=result[:], in_=acc[:])
            nc.sync.dma_start(out=out[:, cols], in_=result[:])

        larger(0)
        larger(1)
        quantise(0)
        finish(0, 1, "y_0_%d" % BOTH, nc.scalar.copy)
        larger(3)
        quantise(1)
        finish(1, 1, "y_1_%d" % BOTH, nc.scalar.copy)
        larger(BOTH)
        quantise(3)
        finish(3, 1, "y_0_0", nc.scalar.copy)
        quantise(BOTH)
        finish(BOTH, 1, "y_0_1", nc.vector.tensor_copy)
